import numpy as np, ml_dtypes
CORES = [40,41,42,43,44,45,46,47]
N = 8
BF = ml_dtypes.bfloat16
def gentries(a):
    return np.ascontiguousarray(a.reshape(8, 16, -1).transpose(0, 2, 1)).reshape(8, -1)
def gtable(e):
    e = np.asarray(e); return np.ascontiguousarray(e.reshape(8, -1, 16).transpose(0, 2, 1)).reshape(128, -1).astype(np.int32)
V, L, A, S, C, RO = 8192, 1024, 512, 192, 8, 2
def ringed(o, s):
    n = np.empty(V, np.int64); f = np.roll(o, -1); f[np.append(s[1:], V) - 1] = o[s]; n[o] = f
    return n
def longrings(rng):
    n = np.empty((N, 8, V), np.int64)
    for q in range(N):
        for g in range(8):
            m = int(rng.integers(1, 7)); s = (1 + rng.permutation(15)[:m - 1]) * (V // 16) + rng.integers(0, V // 32, m - 1)
            n[q, g] = ringed(rng.permutation(V), np.sort(np.concatenate([np.zeros(1, np.int64), s])))
    return n
def parts(rng):
    lev = np.array([64, 128, 256], np.float32)
    x = (rng.random((N, 8, 16, V), dtype=np.float32) * rng.choice(lev, (N, 8, 1, V))).astype(np.int32)
    z = (rng.random((N, 8, 16, L), dtype=np.float32) * rng.choice(lev, (N, 8, 1, L))).astype(np.int32)
    w = rng.integers(0, 256, (N, 8, 16, 1)); w[:, :, 0] |= 1
    return x, z, w
def turns(z, w):
    return 1 + (np.sum(w * z, axis=2) & (C - 1))
def stand(n, u, c):
    back = np.argsort(n, axis=-1)
    for i in range(C): u = np.where(i < c, np.take_along_axis(back, u, 2), u)
    return u
def pack(x, z, w, n, c):
    return {"cards": x.reshape(N, 128, V).astype(np.float32).astype(BF), "z0": z.reshape(N, 128, L).astype(np.float32).astype(BF), "wt": np.ascontiguousarray(w.reshape(N, 128, 1)).astype(np.int32),
            "cur": np.stack([gtable(a) for a in c]), "nx": n.astype(np.int32)}
def setup_inputs(rng):
    x, z, w = parts(rng); size = rng.permutation(np.tile(np.array([V, 2 * A, A // 2, A // 4]), 2 * N)).reshape(N, 8, 1)
    pool = np.argsort(rng.random((N, 8, V)), axis=-1)
    return pack(x, z, w, longrings(rng), np.take_along_axis(pool, (rng.random((N, 8, L)) * size).astype(np.int64), 2))
def setup_inputs_room(rng):
    x, z, w = parts(rng); n = longrings(rng); u = np.empty((N, 8, L), np.int64)
    many = rng.choice(np.array([0, 2, S - 2, S, S + 2, A]), (N, 8)); many[0] = (S, S + 2, A, S - 2, 2, 0, S, S + 2)
    for g, m in enumerate((S, S, S - 2, S + 2, A, A, 0, 2)): many[1 + g % (N - 1), (g + 1) % 8] = m
    w[0, 2] = 0
    for q in range(N):
        for g in range(8):
            p = rng.permutation(V); k = p[:A].reshape(A // 2, 2).copy(); rest = rng.permutation(A // 2)[int(many[q, g]) // 2:]
            if (q, g) == (0, 5):
                k[np.arange(A // 2), rng.integers(0, 2, A // 2)] = p[A]; k[int(rng.integers(0, A // 2))] = p[A]
            else:
                b = int(rng.integers(0, len(rest) // 2 + 1)); k[rest[b:2 * b], 0] = k[rest[:b], 1]; k[rest[2 * b:], 1] = k[rest[2 * b:], 0]
            u[q, g] = np.concatenate([k.reshape(-1), p[rng.integers(0, 2 * A, L - A)]])
    return pack(x, z, w, n, stand(n, u, turns(z, w)))
def setup_inputs_ties(rng):
    x, z, w = parts(rng); i = np.arange(16).reshape(1, 1, 16, 1)
    h = ((5 * i + rng.integers(0, 16, (N, 8, 1, V))) & 15) < rng.integers(7, 11, (N, 8, 1, V))
    x[:, ::2] = np.where(h, 255, 0)[:, ::2]; z[:, ::2] = np.minimum(z[:, ::2], 254)
    base = rng.choice(np.array([0, 100, 253]), (N, 4, 1, 1)); base[0, :, 0, 0] = (0, 100, 253, 0)
    x[:, 1::2] = base + rng.integers(0, 3, (N, 4, 16, V)); z[:, 1::2] = base + rng.integers(0, 2, (N, 4, 16, L))
    w[:, 2] = 0; w[:, 3] = 255; w[:, 4] = C * rng.integers(0, 256 // C, (N, 16, 1)); w[:, 5, 1:] = 0
    w[:, 7] = 0; w[:, 7, 0] = 1; z[:, 7, 0] |= C - 1
    return pack(x, z, w, longrings(rng), rng.integers(0, V, (N, 8, L)))
def setup_inputs_close(rng):
    x, z, w = parts(rng); n = np.empty((N, 8, V), np.int64); u = np.empty((N, 8, L), np.int64)
    w[:, 3::4, 0] = 1; w[:, 3::4, 1:] = C * rng.integers(0, 256 // C, (N, 2, 15, 1)); z[:, 3::4, :8, :A] = 255
    for q in range(N):
        for g in range(8):
            o = rng.permutation(V); a = int(rng.integers(0, V)); k = rng.permutation(A)
            if g % 4 == 0:
                o = np.arange(V); a = 1024 * int(rng.integers(0, V // 1024)) + int(rng.integers(240, 273))
            if g % 4 == 1: k = np.arange(A)
            if g % 4 == 3:
                t = 2 * rng.permutation(A // 2).reshape(2, A // 4); k = np.stack([t[0], t[1], t[0] + 1, t[1] + 1], axis=1).reshape(-1)
                i = o[(a + t[0] + 1) % V]; x[q, g, 0, i] = (x[q, g, 0, i] | (C - 1)) - 1
                i = o[(a + t[1] + 2) % V]; x[q, g, 0, i] = x[q, g, 0, i] | (C - 1)
            n[q, g] = ringed(o, np.zeros(1, np.int64))
            u[q, g] = o[(a + np.concatenate([k, rng.integers(-2 * C, A, L - A)])) % V]
    return pack(x, z, w, n, stand(n, u, turns(z, w)))
def setup_inputs_rings(rng):
    x, z, w = parts(rng); n = np.empty((N, 8, V), np.int64); c = rng.integers(0, V, (N, 8, L))
    for q in range(N):
        for g in range(8):
            m = (1, 2, 3, C, C + 1, 0, V, 7)[(q + g) % 8]; o = np.arange(V) if m == V else rng.permutation(V)
            n[q, g] = ringed(o, np.arange(0, V, m) if m > 0 else np.unique(np.concatenate([np.zeros(1, np.int64), rng.integers(0, V, V // 8)])))
    c[:, :, :8] = rng.choice(np.array([0, V - 1]), (N, 8, 8)); c[:, :, A - 2] = 0; c[:, :, A - 1] = V - 1; c[:, :, A] = 0; c[:, :, L - 1] = V - 1
    return pack(x, z, w, n, c)
def setup_inputs_spread(rng):
    x, z, w = parts(rng)
    def uneven(k):
        a = np.minimum((np.exp2(8 * rng.random((N, 8, 1, k))) * rng.random((N, 8, 16, k), dtype=np.float32)).astype(np.int32), 255); e = rng.random((N, 8, 1, k))
        return np.where(e < 0.04, 0, np.where(e > 0.96, 255, a))
    x = uneven(V); z = uneven(L); w = np.minimum(np.exp2(8 * rng.random((N, 8, 16, 1))).astype(np.int64), 255)
    return pack(x, z, w, longrings(rng), (V * rng.random((N, 8, L)) ** 3).astype(np.int64))
def check_inputs(d):
    bad = []
    for k in ("cards", "z0"):
        a = d[k].astype(np.float32)
        if not (np.min(a) >= 0 and np.max(a) <= 255 and np.all(np.floor(a) == a)): bad.append("whole numbers of " + k)
    for k, hi in (("wt", 255), ("cur", V - 1)):
        if np.min(d[k]) < 0 or np.max(d[k]) > hi: bad.append("range of " + k)
    if not np.all(np.sort(d["nx"], axis=-1) == np.arange(V)): bad.append("each row of nx holds every card once")
    return bad
def reference(cards, z0, wt, cur, nx):
    x = cards.astype(np.float32).astype(np.int32).reshape(N, 8, 16, V); z = z0.astype(np.float32).astype(np.int32).reshape(N, 8, 16, L)
    w = wt.astype(np.int32).reshape(N, 8, 16, 1); nxt = nx.astype(np.int64); v = np.stack([gentries(a) for a in cur]).astype(np.int64)
    for rnd in range(RO):
        c = 1 + (np.sum(w * z, axis=2) & (C - 1))
        for s in range(C):
            go = s < c
            v = np.where(go, np.take_along_axis(nxt, v, 2), v)
            cd = np.take_along_axis(x, v[:, :, None, :], 3)
            up = go & (np.add.reduce((cd > z).astype(np.int32), axis=2) >= 9)
            z = np.where(up[:, :, None, :], (z + cd) >> 1, z)
        u = v; v = np.take_along_axis(nxt, u, 2)
        z = np.abs(z - np.take_along_axis(x, v[:, :, None, :], 3))
        a = u[:, :, :A]; b = v[:, :, :A]
        key = np.arange(N * 8).reshape(N, 8, 1) * V + a
        cnt = np.bincount(key.reshape(-1), minlength=N * 8 * V).reshape(N, 8, V)
        alone = (np.take_along_axis(cnt, a, 2) == 1).reshape(N, 8, A // 2, 2)
        cut = np.repeat(np.all(alone, axis=3), 2, axis=2)
        i, g, j = np.nonzero(cut)
        nxt[i, g, a[i, g, j]] = b[i, g, j ^ 1]
        if rnd < RO - 1:
            top = [[b[q, h][cut[q, h]][:S] for h in range(8)] for q in range(N)]
            sent = [[x[q, h][:, top[q][h]] for h in range(8)] for q in range(N)]
            for q in range(N):
                for h in range(8):
                    r = (q + 1 + (h + rnd) % (N - 1)) % N; k = (h + 1) % 8; m = min(len(top[q][h]), len(top[r][k]))
                    x[r, k][:, top[r][k][:m]] = sent[q][h][:, :m]
    return {"yz": z.reshape(N, 128, L).astype(np.float32).astype(BF), "yc": v.astype(np.float32), "yn": nxt.astype(np.float32)}

@@ -1,0 +1,497 @@
+from concourse.bass import DstId, RemoteDMATransfer
+from concourse.mybir import AluOpType as A, ActivationFunctionType as F
+
+V, L, AC, S, W = 8192, 1024, 512, 192, 208
+BF, F32, I32, U16, F16 = "bfloat16", "float32", "int32", "uint16", "float16"
+SCRATCH = {}
+for _dt, _bufs in (
+        (BF, dict(cw=V + S + 128, nt=V + AC + 128, nhi=512, nlo=512, zz=3 * L, gch=2 * L, g2=2 * L, g3=AC, db=L, bb=L, fs=128,
+                  cq=128, pen=1024, hl=64, ohh=32 * 128, ohl=32 * 66, fl=520, cut=32, s1=32, cp=L + 128, sb=W, land=7 * W, ar=W,
+                  tib=128, tih=66, zs=144, zc=144, zw=144, zq=144, zp=144, idp=128, idn=128, bd=128, selt=1024, ua=128,
+                  ub=128, un=128, sa=128, sh=128, shd=7 * 128, one=32)),
+        (F16, dict(cd=18 * L, dd=L)),
+        (I32, dict(nxi=512, curi=64, wti=1, rr=L, ci=192, cj=192, ui=32, uj=64, pi=8)),
+        (U16, dict(xo=19 * 64, uo=64, o1=32, o2=32, o3=12, to=12)),
+        (F32, dict(eq=512, pr=512, l4=128, cs=520, t1=32, t2=32, tf=12, cnt=2, t3=12, t4=12, t5=12, pf=16, ti=144, di=128,
+                   tg=128, jj=32, j8=32, jm=32, idf=128, swf=128, q4=4, rs=32))):
+    for _k in _bufs:
+        SCRATCH[_k] = ("sbuf", [128, _bufs[_k]], _dt)
+PSUM = ["pd0", "pd1", "pf0", "pf1", "pch", "pm1", "pm2", "phb"]
+for _k in PSUM:
+    SCRATCH[_k] = ("psum", [128, 512], F32)
+SEMAPHORES = ["qV", "qS", "qP", "qG", "arr", "sent"] + ["d%d" % i for i in range(24)]
+
+CY, PC, GA, SCA, WAKE = 1.04, 0.55, 1.56, 3.8, 100.0
+P = {'ch': [['SV', 'SV', 'SV', 'SV', 'S', 'SS', 'S', 'SS'], ['S', 'S', 'S', 'S', 'S', 'S', 'S', 'S']],
+     'bs': ['VVVVVVVVVVVSVVVV', 'VVVVVVVVVVSVVSSV'], 'd1': 'VS', 'cg': ['SSSSSSSSSSSSSSSSSS', 'SSSSSSSSSSSSSSSSSS'],
+     'oh': ['SSSSSSSS', 'SSSSSSSS'], 'g2': ['SS', 'SS'], 'ev': 'NN'}
+URGE = 'a:438 c01:381 c02:490 c03:568 c04:829 c05:527 c06:742 c07:108 c08:633 c11:7 c12:37 c13:95 c14:-172 c15:-274 c16:19 c17:519 c18:32 d0:20 d1:1 h00:336 h01:331 h10:92 h11:90 k010:188 k011:217 k020:174 k021:134 k030:34 k031:9 k040:78 k041:12 k050:29 k051:-46 k060:7 k061:41 k070:341 k071:1 k080:-168 k081:-407 k090:-6 k091:-56 k110:140 k111:26 k120:44 k121:29 k130:-21 k131:-23 k140:-5 k141:-17 k150:-38 k151:-39 k160:-48 k161:-31 k170:-26 k171:-101 k180:143 k181:-55 k190:70 k191:-133 sl:5 sm:127 t0:35 t1:-6 u0:157 u1:126 v0:18 v1:-577 w000:-121 w001:-175 w010:-12 w011:-405 w020:-196 w021:-139 w030:-52 w031:-186 w040:50 w041:-44 w050:-26 w051:-79 w060:-62 w061:45 w070:42 w071:-233 w080:-198 w081:-187 w100:234 w101:870 w110:542 w111:112 w120:535 w121:296 w130:607 w131:260 w140:302 w141:12 w150:24 w151:456 w160:471 w161:488 w170:368 w171:578 w180:216 w181:258 x0:153 x1:-216 y:-182'
+ORDER = {}
+
+
+def build(T, send):
+    ops, tag = [], ["a"]
+
+    def R(name, a=0, b=None):
+        return (name, a, (SCRATCH[name][1][1] if name in SCRATCH else 1) if b is None else b)
+
+    def add(q, fn, rd, wr, cost, kind="c", lat=0.0, pri=0.0):
+        rd, wr = ([R(x) if isinstance(x, str) else x for x in l] for l in (rd, wr))
+        ops.append(dict(q=q, fn=fn, rd=rd, wr=wr, cost=cost, kind=kind, lat=lat, pri=pri, tag=tag[0],
+                        banks=sorted(set(r[0] for r in rd + wr if r[0] in PSUM))))
+
+    def ap(r):
+        return T[r[0]][:, r[1]:r[2]]
+
+    def vc(i, f=1.0):
+        return 55 + max(8, (i[2] - i[1]) * f) * CY
+
+    def two(*rs):
+        return 0.5 if all(SCRATCH[r[0]][2] in (BF, F16, U16) for r in rs) else 1.0
+
+    def cols(x):
+        return [x] if isinstance(x, tuple) else []
+
+    def sval(x):
+        return ap(x) if isinstance(x, tuple) else x
+
+    def ts(o, i, s1, s2, op0, op1=None):
+        def fn(g):
+            if op1 is None:
+                return g.vector.tensor_scalar(ap(o), ap(i), sval(s1), None, op0)
+            return g.vector.tensor_scalar(ap(o), ap(i), sval(s1), sval(s2), op0, op1)
+        add("V", fn, [i] + cols(s1) + cols(s2), [o], vc(i, two(o, i)))
+
+    def tt(o, a, b, op):
+        add("V", lambda g: g.vector.tensor_tensor(ap(o), ap(a), ap(b), op), [a, b], [o],
+            vc(a, 1.0 if (a[0] in PSUM or b[0] in PSUM) else 2.0))
+
+    def cp(o, i):
+        add("V", lambda g: g.vector.tensor_copy(ap(o), ap(i)), [i], [o], vc(i, two(o, i)))
+
+    def ms(o, val, wr=None):
+        add("V", lambda g: g.vector.memset(ap(o), val), [], wr or [o], vc(o, two(o)))
+
+    def act(o, i, func, bias=0.0, scale=1.0, rd=None, wr=None):
+        add("S", lambda g: g.scalar.activation(ap(o), ap(i), func, bias=sval(bias), scale=sval(scale)),
+            (rd or [i]) + cols(bias) + cols(scale), wr or [o], 65 + (i[2] - i[1]) * CY)
+
+    def gather(q, o, win, off, rd, bias=None):
+        def fn(g):
+            src = ap(win).indirect(ap(off))
+            if q == "S":
+                return g.scalar.activation(ap(o), src, F.Identity, bias=bias or 0.0)
+            if bias is None:
+                return g.vector.tensor_copy(ap(o), src)
+            return g.vector.tensor_scalar(ap(o), src, bias, None, A.add)
+        add(q, fn, rd + [off], [o], 60 + (o[2] - o[1]) * GA * CY)
+
+    def scatter(win, off, i, wr):
+        add("V", lambda g: g.vector.tensor_copy(ap(win).indirect(ap(off)), ap(i)), [off, i], wr, 50 + (i[2] - i[1]) * SCA * CY)
+
+    def iota(o, pat, base, cm, wr=None):
+        kw = {} if SCRATCH[o[0]][2] == I32 else dict(allow_small_or_imprecise_dtypes=True)
+        add("G", lambda g: g.iota(ap(o), pat, base, cm, **kw), [], wr or [o], 130 + 2 * (o[2] - o[1]) * CY)
+
+    def sel(o, i, base, op, fill, pat=((-1, 128),), cm=1):
+        add("G", lambda g: g.affine_select(ap(o), ap(i), [list(x) for x in pat], op, fill, base, cm), [i], [o], 170 + 256 * CY)
+
+    def mm(groups, first=True, last=True):
+        rd, wr, cost = [], [], 60.0
+        for o, terms in groups:
+            wr.append(o)
+            for l, r, st in terms:
+                rd += [l, r]
+                cost += max(64, o[2] - o[1]) * PC * (4 if SCRATCH[l[0]][2] == F32 else 1)
+
+        def fn(g):
+            ins = None
+            for o, terms in groups:
+                for k, (l, r, st) in enumerate(terms):
+                    rhs = ap(r) if st == 1 else T[r[0]][:, r[1]:r[2]:st]
+                    ins = g.tensor.matmul(ap(o), ap(l), rhs, first and k == 0, last and k == len(terms) - 1)
+            return ins
+        add("P", fn, rd, wr, cost)
+
+    def dma(q, pairs, rd, wr, nbytes, pri=0.0, **kw):
+        def fn(g, sem):
+            e = g if q == "G" else (g.sync if q == "Y" else g.scalar)
+            for o, i in pairs:
+                e.dma_start(o, i, **kw).then_inc(sem, 16)
+            return 16 * len(pairs)
+        add(q, fn, rd, wr, (600 if q == "G" else 100) * len(pairs), kind="d", lat=1800 + nbytes / 250.0, pri=pri)
+
+    def blk(name, k, n=128):
+        return R(name, n * k, n * k + n)
+
+    def wrap(z, src, a, b):
+        return [(R(z, 15 - i, 143 - i), R(src, a + i, b), 16) for i in range(16)]
+
+    NT = ["ntA", "ntB", "ntC", "ntD"]
+    CW = ["cwA", "cwB"]
+    dma("Y", [(T.nxi[:], T.nx[:])], [], ["nxi"], 1 << 18, pri=1e5)
+    dma("S", [(T.curi[:], T.cur[:])], [], ["curi"], 1 << 15, pri=1e5)
+    dma("S", [(T.wti[:], T.wt[:])], [], ["wti"], 512, pri=1e5)
+    dma("S", [(T.zz[:, 0:L], T.z0[:])], [], [R("zz", 0, L)], 1 << 18, pri=1e5)
+    dma("Y", [(T.cw[:, 0:V // 2], T.cards[:, 0:V // 2])], [], ["cwA"], 1 << 20, pri=5e4)
+    ms(R("nt", 0, 1536), 0.0, ["f0"])
+    ms(R("nt", 1536, 3840), 0.0, ["f1"])
+    act(R("nt", 3840, 5376), R("nt", 0, 1536), F.Copy, rd=["f0"], wr=["f2"])
+    act(R("nt", 5376, 6912), R("nt", 0, 1536), F.Copy, rd=["f0"], wr=["f4"])
+    iota(R("pi", 0, 1), [[0, 1]], 0, 1)
+    iota(R("ti"), [[1, 144]], 0, 0)
+    iota(R("nt", 6912, V), [[0, V - 6912]], 0, 0, ["f3"])
+    cp(R("nhi"), R("nxi"))
+    tt(R("nlo"), R("nxi"), R("nhi"), A.subtract)
+    zr = ["f1", "f2", "f3", "f4"]
+    dma("Y", [(T.nt[0:128:16, 0:V], T.nhi[:])], ["nhi"] + zr, ["ntA", "f0"], 1 << 17)
+    dma("Y", [(T.nt[1:128:16, 0:V], T.nlo[:])], ["nlo"] + zr, ["ntB", "ntC", "ntD"], 1 << 17)
+    dma("Y", [(T.cw[:, V // 2:V], T.cards[:, V // 2:V])], ["nlo"] + zr, ["cwB"], 1 << 20, pri=-1e5)
+    cp(R("xo", 0, 64), R("curi"))
+    ts(R("pi", 1, 2), R("pi", 0, 1), 15, None, A.bitwise_and)
+    ts(R("pi", 2, 3), R("pi", 0, 1), 4, None, A.logical_shift_right)
+    ts(R("pi", 3, 4), R("pi", 0, 1), 1, None, A.bitwise_and)
+    ts(R("pi", 4, 5), R("pi", 0, 1), 3, None, A.bitwise_and)
+    ts(R("pi", 5, 6), R("pi", 0, 1), 15, 2, A.bitwise_and, A.logical_shift_right)
+    cp(R("pf", 0, 6), R("pi", 0, 6))
+    ic, gi, par, p3, qc, g16, lo2, sw, cc, r2, wf = (R("pf", k, k + 1) for k in range(1, 12))
+    ts(g16, gi, 16.0, None, A.mult)
+    ts(lo2, ic, 1.5, None, A.is_lt)
+    ts(R("zs"), R("ti"), 15.0, g16, A.subtract, A.is_equal)
+    ts(R("zc"), R("zs"), lo2, None, A.mult)
+    cp(wf, R("wti"))
+    act(R("zw"), R("zs"), F.Identity, scale=wf)
+    iota(R("di"), [[1, 128]], 0, -1)
+    iota(R("tg"), [[16, 8], [0, 16]], 0, 0)
+    iota(R("jj"), [[16, 32]], 0, 1)
+    iota(R("j8"), [[16, 32]], V, 1)
+    iota(R("jm"), [[16, 32]], -1535, 1)
+    ms(R("cp", 0, S), 0.0)
+    zero = R("cp", 0, 128)
+    idp, idn, idf, bd = R("idp"), R("idn"), R("idf"), R("bd")
+    sel(idp, zero, 0, A.not_equal, 1.0)
+    sel(idn, zero, 0, A.not_equal, -1.0)
+    sel(R("sa"), zero, 16, A.not_equal, 1.0)
+    sel(R("sh"), R("sa"), -112, A.not_equal, 1.0)
+    act(idf, idp, F.Copy)
+    ts(bd, R("tg"), g16, None, A.is_equal)
+    for i in range(8):
+        sel(blk("selt", i), zero, -i, A.not_equal, 1.0, ((-16, 8), (0, 16)))
+    ts(R("tih"), R("ti", 0, 66), -0.5, None, A.add)
+    ts(sw, par, -2.0, 1.0, A.mult, A.add)
+    ts(R("swf"), R("di"), sw, None, A.is_equal)
+    ts(cc, gi, 4.0, p3, A.mult, A.add)
+    ts(R("rs"), R("ti", 0, 32), cc, None, A.is_equal)
+    ts(R("q4"), R("ti", 0, 4), qc, None, A.is_equal)
+    act(R("tib"), R("ti", 0, 128), F.Copy)
+    ts(r2, ic, 2.0, 16384.0, A.is_equal, A.mult)
+    tt(R("zq", 0, 143), R("zs", 0, 143), R("zs", 1, 144), A.add)
+    act(R("zp", 0, 143), R("zq", 0, 143), F.Identity, scale=r2)
+    act(R("ua"), bd, F.Identity, scale=-1.0)
+    sel(R("ub"), R("ua"), 0, A.is_ge, 0.0)
+    sel(R("un"), R("ub"), 0, A.not_equal, -2048.0)
+    for d in range(7):
+        sel(blk("shd", d), R("sh"), d + 1, A.is_equal if d else A.is_ge, 0.0, ((-1, 8), (0, 16)), 0)
+    ms(R("one"), 1.0)
+    ms(R("sb", S, W), 0.0)
+
+    def xo(r, s, h=None):
+        return blk("xo", 9 * r + s, 64) if h is None else blk("xo", 18 * r + 2 * s + h, 32)
+
+    def cd(r, s, h):
+        return blk("cd", 18 * r + 2 * s - 2 + h, 512)
+
+    def zz(r, h):
+        return blk("zz", 2 * r + h, 512)
+
+    def chase(r):
+        for s in range(1, 9):
+            b, tag[0], e = L * (s % 2), "c%d%d" % (r, s), P["ch"][r][s - 1]
+            if len(e) == 2:
+                for h in range(2):
+                    gather(e[h], R("gch", b + 512 * h, b + 512 * h + 512), R("nt", 0, V), xo(r, s - 1, h), NT)
+            else:
+                gather(e, R("gch", b, b + L), R("nt", 0, V), xo(r, s - 1), NT)
+            mm([(blk("pch", s - 1, 64), wrap("zc", "gch", b, b + L))])
+            cp(xo(r, s), blk("pch", s - 1, 64))
+
+    def cards(r, steps):
+        for s in steps:
+            for h in range(2):
+                tag[0] = "k%d%d%d" % (r, s, h)
+                gather(P["cg"][r][2 * s - 2 + h], cd(r, s, h), R("cw", 0, V), xo(r, s, h), CW, bias=0.25 * min(s, 8))
+
+    def turns(r):
+        tag[0] = "t%d" % r
+        gs = [(R("pm1", 128, 192), wrap("zw", "zz", L * r, L * r + L))]
+        for h in range(2):
+            gs.append((blk("pm1", 3 + h, 64), [(R("zw", 15 - i, 143 - i), blk("zz", 16 * r + 8 * h + i, 64), 1) for i in range(8)]))
+        mm(gs)
+        cp(R("ci"), R("pm1", 128, 320))
+        ts(R("cj"), R("ci"), 7, None, A.bitwise_and)
+        cp(R("cq"), R("cj", 64, 192))
+        for s in range(1, 8):
+            act(blk("pen", s), R("cq"), F.Relu, bias=32.0 * s, scale=-32.0)
+        for s in range(8):
+            ts(blk("eq", s, 64), R("cj", 0, 64), float(s), None, A.is_equal)
+
+    def cuts(r):
+        g2, tag[0] = L * r, "u%d" % r
+        for s in range(8):
+            tt(blk("pr", s, 64), blk("eq", s, 64), blk("pch", s, 64), A.mult)
+            mm([(R("pm1", 0, 64), [(idf, blk("pr", s, 64), 1)])], s == 0, s == 7)
+        for a in range(4):
+            ts(blk("l4", a, 32), R("pm1", 0, 32), R("q4", a, a + 1), None, A.mult)
+        cp(R("uo"), R("pm1", 0, 64))
+        mm([(R("pm1", 64, 96), [(R("l4"), R("rs"), 1)])])
+        cp(R("ui"), R("pm1", 64, 96))
+        ts(R("uj", 0, 32), R("ui"), 6, None, A.logical_shift_right)
+        ts(R("uj", 32, 64), R("ui"), 63, None, A.bitwise_and)
+        cp(R("hl"), R("uj"))
+
+        def reveal():
+            tag[0] = "v%d" % r
+            for h in range(2):
+                gather(P["g2"][r][h], blk("g2", 2 * r + h, AC), R("nt", 0, V), blk("uo", h, 32), NT)
+            mm([(R("pm2", 0, 64), wrap("zc", "g2", g2, g2 + L))])
+            cp(xo(r, 9), R("pm2", 0, 64))
+
+        early = P["ev"][r] == "Y"
+        if early:
+            reveal()
+        for k in range(2):
+            bank, h0, step = ("phb", "pm2")[k], 128 * k, P["oh"][r][4 * k] == "S"
+            w, tag[0] = 65 if step else 64, "h%d%d" % (r, k)
+            for gq in range(4 * k, 4 * k + 4):
+                for c in range(4 * gq, 4 * gq + 4):
+                    ts(blk("ohh", c), R("tib"), R("hl", c, c + 1), None, A.is_equal)
+                    if step:
+                        act(R("ohl", 66 * c, 66 * c + w), R("tih", 0, w), F.Sign, bias=R("hl", 32 + c, 33 + c), scale=-1.0)
+                    else:
+                        ts(R("ohl", 66 * c, 66 * c + w), R("tib", 0, w), R("hl", 32 + c, 33 + c), None, A.is_equal)
+                a = h0 + w * (gq % 4)
+                mm([(R(bank, a, a + w), [(blk("ohh", c), R("ohl", 66 * c, 66 * c + w), 1) for c in range(4 * gq, 4 * gq + 4)])])
+            f0 = 260 * k
+            if step:
+                act(R("cs", f0, f0 + 260), R(bank, h0, h0 + 260), F.Identity, bias=3.0)
+                tt(R("fl", f0, f0 + 259), R(bank, h0, h0 + 259), R("cs", f0 + 1, f0 + 260), A.is_gt)
+            else:
+                act(R("fl", f0, f0 + 256), R(bank, h0, h0 + 256), F.Relu, bias=-1.0)
+            dma("Y", [(T.nt[64 * k + 16 * j + 2:64 * k + 16 * j + 3, 0:V], T.fl[:, f0 + w * j:f0 + w * j + 64]) for j in range(4)],
+                [R("fl", f0, f0 + 260)], [NT[2 + k]], 1 << 16)
+        if early:
+            tag[0] = "x%d" % r
+            gather("S", R("g3"), R("nt", 0, V), R("uo", 0, 32), NT)
+        else:
+            reveal()
+        tag[0], (m0, m1) = "x%d" % r, ("g3", 0) if early else ("g2", g2)
+        mm([(R("pm1", 96, 128), [(R("swf"), blk("l4", a, 32), 1) for a in range(4)]
+             + [(R("zp", 14 - (i & 14), 142 - (i & 14)), R(m0, m1 + i, m1 + AC), 16) for i in range(16)])])
+        tt(R("t1"), R("j8"), R("pm1", 96, 128), A.min)
+        cp(R("o1"), R("t1"))
+        if r == 0:
+            ts(R("cut"), R("pm1", 96, 128), float(V), None, A.is_lt)
+        scatter(R("nt"), R("o1"), R("g2", g2, g2 + AC), NT)
+
+    def deal():
+        tag[0] = "d0"
+        add("V", lambda g: g.vector.tensor_tensor_scan(T.s1[:], T.one[:], T.cut[:], 0.0, A.mult, A.add),
+            ["one", "cut"], ["s1"], vc(R("s1")))
+        mm([(R("pm2", 64, 96), [(bd, R("s1"), 1), (R("un"), R("cut"), 1)]), (R("pm2", 96, 97), [(bd, R("s1", 31, 32), 1)])])
+        tt(R("t2"), R("jm"), R("pm2", 64, 96), A.min)
+        ts(R("o2"), R("t2"), 2047.0, None, A.add)
+        ts(R("cnt", 0, 1), R("pm2", 96, 97), float(S), None, A.min)
+        cp(R("sb", S, S + 1), R("cnt", 0, 1))
+        scatter(R("cp"), R("o2"), R("g2", 0, AC), ["cp"])
+        mm([(R("pm2", 100, 112), wrap("zc", "cp", 0, S))])
+        cp(R("to"), R("pm2", 100, 112))
+        cp(R("tf"), R("pm2", 100, 112))
+        gather("S", R("sb", 0, S), R("cw", 0, V), R("to"), CW)
+        add("G", send, ["sb"], ["land"], 1000, kind="r", lat=4500)
+        tag[0] = "d1"
+        mm([(R("phb", 0, W), [(blk("shd", d), blk("land", d, W), 1) for d in range(7)])])
+        act(R("ar"), R("phb", 0, W), F.Copy)
+        ts(R("cnt", 1, 2), R("ar", S, S + 1), R("cnt", 0, 1), g16, A.min, A.add)
+        ts(R("t3"), R("jj", 0, 12), R("cnt", 1, 2), 16384.0, A.is_ge, A.mult)
+        tt(R("t4"), R("t3"), R("tf"), A.add)
+        tt(R("t5"), R("t4"), R("j8", 0, 12), A.min)
+        cp(R("o3"), R("t5"))
+        scatter(R("cw"), R("o3"), R("ar", 0, S), CW)
+
+    def walk(r):
+        for h in range(2):
+            pd, tag[0] = R("pd%d" % h), "w%d0%d" % (r, h)
+            mm([(pd, [(idp, cd(r, 1, h), 1), (idn, zz(r, h), 1)])])
+            if P["d1"][r] == "S":
+                act(blk("dd", h, 512), pd, F.Copy)
+            else:
+                cp(blk("dd", h, 512), pd)
+        for s in range(1, 9):
+            for h in range(2):
+                pd, pf, tag[0] = R("pd%d" % h), "pf%d" % h, "w%d%d%d" % (r, s, h)
+                d, b, rr, fs = blk("dd", h, 512), blk("bb", h, 512), blk("rr", h, 512), blk("fs", h, 64)
+                on_s = P["bs"][r][2 * s - 2 + h] == "S"
+                if on_s:
+                    act(b, d, F.Sign, bias=-0.5)
+                else:
+                    ts(b, d, 0.5, None, A.is_gt)
+                pen = [(idn, blk("pen", 2 * s - 2 + h, 64), 1)] if s > 1 else []
+                mm([(R(pf, 0, 64), pen + [(R("zs", 15 - i, 143 - i), blk("bb", 8 * h + i, 64), 1) for i in range(8)])])
+                ts(fs, R(pf, 0, 64), 1.0 if on_s else 8.5, 0.5, A.is_lt, A.max)
+                mm([(blk(pf, i, 64), [(blk("selt", i), fs, 1)]) for i in range(8)])
+                mm([(pd, [(idp, cd(r, s + 1, h), 1), (idn, cd(r, s, h), 1)])])
+                tt(rr, d, R(pf), A.mult)
+                if s < 8:
+                    tt(d, rr, pd, A.add)
+                else:
+                    tt(blk("db", h, 512), rr, pd, A.add)
+                    act(zz(r + 1, h), blk("db", h, 512), F.Abs)
+                    if r == 1:
+                        dma("Y", [(T.yz[:, 512 * h:512 * h + 512], ap(zz(2, h)))], [zz(2, h)], ["yz%d" % h], 1 << 17)
+
+    turns(0)
+    chase(0)
+    cards(0, range(1, 9))
+    cuts(0)
+    cards(0, [9])
+    deal()
+    chase(1)
+    walk(0)
+    turns(1)
+    cards(1, range(1, 9))
+    cuts(1)
+    cards(1, [9])
+    tag[0] = "y"
+    dma("G", [(T.yn[:], T.nt[0:128:16, 0:V])], NT, ["yn"], 1 << 18)
+    dma("G", [(T.yc[:], T.g2[0:128:16, L:2 * L])], [R("g2", L, 2 * L)], ["yc"], 1 << 15)
+    dma("G", [(T.yn[:], T.nt[1:128:16, 0:V])], NT, ["yn"], 1 << 19, accum_op=A.add, max_dma_last_dim=4096)
+    dma("G", [(T.yc[:], T.g2[1:128:16, L:2 * L])], [R("g2", L, 2 * L)], ["yc"], 1 << 16, accum_op=A.add, max_dma_last_dim=4096)
+    walk(1)
+    return ops
+
+
+def depend(ops):
+    hist, deps = {}, []
+    for n, o in enumerate(ops):
+        ds = set()
+        for kind, rs in (("r", o["rd"]), ("w", o["wr"])):
+            for name, a, b in rs:
+                for m, k2, a2, b2 in hist.get(name, []):
+                    if a < b2 and a2 < b and (kind == "w" or k2 == "w"):
+                        ds.add(m)
+        for kind, rs in (("r", o["rd"]), ("w", o["wr"])):
+            for name, a, b in rs:
+                h = hist.setdefault(name, [])
+                if kind == "w":
+                    h[:] = [e for e in h if not (a <= e[2] and e[3] <= b)]
+                h.append((n, kind, a, b))
+        deps.append(ds)
+    return deps
+
+
+def chains(ops, deps):
+    n = len(ops)
+    succ, tail = [[] for _ in range(n)], [0.0] * n
+    for k in range(n):
+        for m in deps[k]:
+            succ[m].append(k)
+    for k in range(n - 1, -1, -1):
+        tail[k] = ops[k]["cost"] + ops[k]["lat"] + WAKE + max([tail[j] for j in succ[k]] + [0.0])
+    return succ, tail
+
+
+def dispatch(ops, deps, succ, tail, urge):
+    n = len(ops)
+    prio = [tail[k] + ops[k]["pri"] + urge.get(ops[k]["tag"], 0) for k in range(n)]
+    slack, idle = max(0, urge.get("sl", 0) / 10), urge.get("sm", 0) / 300
+    left, at, free, bk, order = [len(d) for d in deps], [0.0] * n, {q: 0.0 for q in "VSPGY"}, {}, []
+    ready = {q: [k for k in range(n) if left[k] == 0 and ops[k]["q"] == q] for q in "VSPGY"}
+    while len(order) < n:
+        bt = None
+        for q in "VSPGY":
+            st = []
+            for k in ready[q]:
+                t = max(at[k], free[q])
+                for b in ops[k]["banks"]:
+                    e = bk.get(b)
+                    if e and e[1] != q and e[0] + WAKE > t:
+                        t = e[0] + WAKE
+                st.append((t, k))
+            if st and (bt is None or min(st)[0] < bt[0]):
+                bt = (min(st)[0], q, st)
+        t0, q, st = bt
+        t, k = max(((t, k) for t, k in st if t <= t0 + slack), key=lambda x: prio[x[1]] - idle * (x[0] - t0))
+        ready[q].remove(k)
+        order.append(k)
+        free[q] = t + ops[k]["cost"]
+        for b in ops[k]["banks"]:
+            bk[b] = (free[q], q)
+        for j in succ[k]:
+            at[j] = max(at[j], free[q] + ops[k]["lat"] + WAKE)
+            left[j] -= 1
+            if left[j] == 0:
+                ready[ops[j]["q"]].append(j)
+    return order
+
+
+def emit(g, T, ops, order, deps):
+    eng = {"V": g.vector, "S": g.scalar, "P": g.tensor, "G": g, "Y": g.sync}
+    count, know, token, last, pos = {}, {q: {} for q in eng}, {}, {}, {k: i for i, k in enumerate(order)}
+    nd = 0
+    for k in order:
+        o = ops[k]
+        q = o["q"]
+        need = list(deps[k])
+        for b in o["banks"]:
+            if b in last and ops[last[b]]["q"] != q:
+                need.append(last[b])
+            last[b] = k
+        for m in sorted(need, key=lambda x: -pos[x]):
+            s, v, seen = token[m]
+            if know[q].get(s, 0) < v:
+                eng[q].wait_ge(T.sem[s], v)
+                for s2 in seen:
+                    know[q][s2] = max(know[q].get(s2, 0), seen[s2])
+        if o["kind"] == "c":
+            s = "q" + q
+            o["fn"](g).then_inc(T.sem[s], 1)
+            v = count.get(s, 0) + 1
+        elif o["kind"] == "d":
+            s = "d%d" % nd
+            nd += 1
+            v = o["fn"](g, T.sem[s])
+        else:
+            s = "arr"
+            v = count["sent"] = o["fn"](g)
+        count[s] = v
+        token[k] = (s, v, dict(know[q], **{s: v}))
+    for s in count:
+        g.sync.wait_ge(T.sem[s], count[s])
+
+
+def rank_program(g, core, T, topo):
+    rank = T.rank_of(core)
+    if rank is None:
+        return
+    n = len(T.cores)
+
+    def send(g):
+        peers = [T.cores[(rank + 1 + d) % n] for d in range(n - 1)]
+        es = topo.engines(core, peers[0])
+        far, near = list(es[0::2]), list(es[1::2])
+        trs = []
+        for d, p in enumerate(peers):
+            pool = far if topo.die(p) != topo.die(core) else near
+            rid, pid, _ = topo.addr(p)
+            trs.append(RemoteDMATransfer(dst_ids=[DstId(rid=rid, pnc=pid)], dma_engine_mask=(1 << pool.pop()) | (1 << pool.pop()),
+                                         remote_sem=T.sem.arr, src=T.sb[:], dst=T.land[:, W * d:W * d + W]))
+        g.remote_dma_fused(trs, local_sem=T.sem.sent)
+        return 2 * len(peers)
+
+    ops = build(T, send)
+    if not ORDER:
+        deps = depend(ops)
+        succ, tail = chains(ops, deps)
+        urge = {x.split(":")[0]: 100 * int(x.split(":")[1]) for x in URGE.split()}
+        ORDER["o"] = (dispatch(ops, deps, succ, tail, urge), deps)
+    emit(g, T, ops, *ORDER["o"])

@@ -2,18 +2,19 @@ from concourse.bass import DstId, RemoteDMATransfer
 from concourse.mybir import AluOpType as A, ActivationFunctionType as F
 
 V, L, AC, S, W = 8192, 1024, 512, 192, 208
+VZ = V + 16
 BF, F32, I32, U16, F16 = "bfloat16", "float32", "int32", "uint16", "float16"
 SCRATCH = {}
 for _dt, _bufs in (
-        (BF, dict(cw=V + S + 128, nt=V + AC + 128, nhi=512, nlo=512, zz=3 * L, gch=2 * L, g2=2 * L, g3=AC, db=L, bb=L, fs=128,
-                  cq=128, pen=1024, hl=64, ohh=32 * 128, ohl=32 * 66, fl=520, cut=32, s1=32, cp=L + 128, sb=W, land=7 * W, ar=W,
-                  tib=128, tih=66, zs=144, zc=144, zw=144, zq=144, zp=144, idp=128, idn=128, bd=128, selt=1024, ua=128,
-                  ub=128, un=128, sa=128, sh=128, shd=7 * 128, one=32)),
-        (F16, dict(cd=18 * L, dd=L)),
-        (I32, dict(nxi=512, curi=64, wti=1, rr=L, ci=192, cj=192, ui=32, uj=64, pi=8)),
-        (U16, dict(xo=19 * 64, uo=64, o1=32, o2=32, o3=12, to=12)),
-        (F32, dict(eq=512, pr=512, l4=128, cs=520, t1=32, t2=32, tf=12, cnt=2, t3=12, t4=12, t5=12, pf=16, ti=144, di=128,
-                   tg=128, jj=32, j8=32, jm=32, idf=128, swf=128, q4=4, rs=32))):
+        (BF, dict(cw=VZ + S + 128, nt=VZ + AC + 128, nhi=512, nlo=512, zz=3 * L, gch=8 * L, g2=2 * L, db=L, bb=L, fs=256,
+                  mk=512, hl=64, ohh=32 * 128, ohl=32 * 66, fl=520, cut=32, s1=32, cp=L + 128, sb=W, land=7 * W, ar=S,
+                  tib=128, tih=66, til=64, zs=144, zc=144, zw=144, zq=144, zp=144, idp=128, idn=128, big=128, bd=128, selt=1024,
+                  zer=128, sc1=256, ua=128, ub=128, un=128, sa=128, sh=128, shd=7 * 128, one=32)),
+        (F16, dict(cd=18 * L, dd=L, z4=L)),
+        (I32, dict(nxi=512, curi=64, wti=1, rr=L, ci=64, cj=64, um=64, uu=64, pi=8)),
+        (U16, dict(xo=19 * 64, xr=8 * 64, uo=64, o1=32, o2=32, o3=12, to=12)),
+        (F32, dict(nf=VZ + AC + 128, vf=AC, mn=64, l4=128, cs=520, t1=32, t2=32, cnt=1, t5=12, pf=16, ti=144, di=128,
+                   tg=128, jj=32, j8=44, jm=32, swf=128, q4=4, rs=32))):
     for _k in _bufs:
         SCRATCH[_k] = ("sbuf", [128, _bufs[_k]], _dt)
 PSUM = ["pd0", "pd1", "pf0", "pf1", "pch", "pm1", "pm2", "phb"]
@@ -21,30 +22,40 @@ for _k in PSUM:
     SCRATCH[_k] = ("psum", [128, 512], F32)
 SEMAPHORES = ["qV", "qS", "qP", "qG", "arr", "sent"] + ["d%d" % i for i in range(24)]
 
-CY, PC, GA, SCA, WAKE = 1.04, 0.55, 1.56, 3.8, 100.0
-P = {'ch': [['SV', 'SV', 'SV', 'SV', 'S', 'SS', 'S', 'SS'], ['S', 'S', 'S', 'S', 'S', 'S', 'S', 'S']],
-     'bs': ['VVVVVVVVVVVSVVVV', 'VVVVVVVVVVSVVSSV'], 'd1': 'VS', 'cg': ['SSSSSSSSSSSSSSSSSS', 'SSSSSSSSSSSSSSSSSS'],
-     'oh': ['SSSSSSSS', 'SSSSSSSS'], 'g2': ['SS', 'SS'], 'ev': 'NN'}
-URGE = 'a:438 c01:381 c02:490 c03:568 c04:829 c05:527 c06:742 c07:108 c08:633 c11:7 c12:37 c13:95 c14:-172 c15:-274 c16:19 c17:519 c18:32 d0:20 d1:1 h00:336 h01:331 h10:92 h11:90 k010:188 k011:217 k020:174 k021:134 k030:34 k031:9 k040:78 k041:12 k050:29 k051:-46 k060:7 k061:41 k070:341 k071:1 k080:-168 k081:-407 k090:-6 k091:-56 k110:140 k111:26 k120:44 k121:29 k130:-21 k131:-23 k140:-5 k141:-17 k150:-38 k151:-39 k160:-48 k161:-31 k170:-26 k171:-101 k180:143 k181:-55 k190:70 k191:-133 sl:5 sm:127 t0:35 t1:-6 u0:157 u1:126 v0:18 v1:-577 w000:-121 w001:-175 w010:-12 w011:-405 w020:-196 w021:-139 w030:-52 w031:-186 w040:50 w041:-44 w050:-26 w051:-79 w060:-62 w061:45 w070:42 w071:-233 w080:-198 w081:-187 w100:234 w101:870 w110:542 w111:112 w120:535 w121:296 w130:607 w131:260 w140:302 w141:12 w150:24 w151:456 w160:471 w161:488 w170:368 w171:578 w180:216 w181:258 x0:153 x1:-216 y:-182'
-ORDER = {}
+TIME = dict(cy=0.85, pc=0.43, ga=1.45, sc=3.2, wake=220.0, same=100.0, dma=1100.0, rate=430.0, send=4500.0,
+            call=dict(V=5.0, S=20.0, P=35.0))
+PLAN = {}
+OPT = dict(raw=3, fuse=0, whole="c1", step="SSSS", parts=((4, 4, 4, 4), (4, 4, 4, 4)))
+URGE = {"Hw0": [6, 0], "Hw1": [5, 0], "a": [323, 0], "c0": [810, 81], "c1": [-2, 0], "d0": [309, 0], "d1": [-20, 0], "h0": [-12, -6],
+        "h1": [-1, 0], "k0": [-10, 1], "k1": [-5, -1], "l1": [255, -13], "m0": [-273, 0], "m1": [4, 0], "n": [120, 0], "t0": [-284, 0],
+        "t1": [306, 0], "u0": [-34, 0], "u1": [21, 0], "v0": [102, 0], "v1": [1125, 0], "w0": [-3, -1], "w1": [-6, 0], "x0": [-249, 0],
+        "x1": [311, 0], "y": [-469, 0]}
+LEAN = {"a": -90, "b0": 2, "b1": 0, "c0": 5, "c1": -5, "d0": -90, "d1": 2, "f0": -2, "f1": 10, "h0": -20, "h1": -20, "k0": -10, "k1": 0,
+        "m0": -90, "m1": -2, "u0": 5, "u1": -20, "v0": -90, "v1": -20, "w0": 2, "w1": 5, "x1": -20}
+TRIES = (100000, 300.0)
 
 
 def build(T, send):
-    ops, tag = [], ["a"]
+    ops, tag, loads = [], ["a"], []
 
     def R(name, a=0, b=None):
         return (name, a, (SCRATCH[name][1][1] if name in SCRATCH else 1) if b is None else b)
 
-    def add(q, fn, rd, wr, cost, kind="c", lat=0.0, pri=0.0):
+    def add(q, fn, rd, wr, size, kind="c", nbytes=0, pri=0.0):
         rd, wr = ([R(x) if isinstance(x, str) else x for x in l] for l in (rd, wr))
-        ops.append(dict(q=q, fn=fn, rd=rd, wr=wr, cost=cost, kind=kind, lat=lat, pri=pri, tag=tag[0],
+        ops.append(dict(on={q: (fn, (tuple(size) + (0, 0, 0, 0))[:5])}, rd=rd, wr=wr, kind=kind, nbytes=nbytes, pri=pri, tag=tag[0],
                         banks=sorted(set(r[0] for r in rd + wr if r[0] in PSUM))))
+
+    def either():
+        o = ops.pop()
+        ops[-1]["on"].update(o["on"])
+        ops[-1]["rd"] += [r for r in o["rd"] if r not in ops[-1]["rd"]]
 
     def ap(r):
         return T[r[0]][:, r[1]:r[2]]
 
     def vc(i, f=1.0):
-        return 55 + max(8, (i[2] - i[1]) * f) * CY
+        return 55, max(8, (i[2] - i[1]) * f)
 
     def two(*rs):
         return 0.5 if all(SCRATCH[r[0]][2] in (BF, F16, U16) for r in rs) else 1.0
@@ -74,35 +85,52 @@ def build(T, send):
 
     def act(o, i, func, bias=0.0, scale=1.0, rd=None, wr=None):
         add("S", lambda g: g.scalar.activation(ap(o), ap(i), func, bias=sval(bias), scale=sval(scale)),
-            (rd or [i]) + cols(bias) + cols(scale), wr or [o], 65 + (i[2] - i[1]) * CY)
+            (rd or [i]) + cols(bias) + cols(scale), wr or [o], (65, i[2] - i[1]))
 
-    def gather(q, o, win, off, rd, bias=None):
-        def fn(g):
+    def move(o, i, bias=0.0):
+        if bias:
+            ts(o, i, bias, None, A.add)
+        else:
+            cp(o, i)
+        act(o, i, F.Identity, bias=bias)
+        either()
+
+    def scaled(o, i, col):
+        ts(o, i, col, None, A.mult)
+        act(o, i, F.Identity, scale=col)
+        either()
+
+    def gather(o, win, off, rd, bias=0.0):
+        def on_v(g):
             src = ap(win).indirect(ap(off))
-            if q == "S":
-                return g.scalar.activation(ap(o), src, F.Identity, bias=bias or 0.0)
-            if bias is None:
-                return g.vector.tensor_copy(ap(o), src)
-            return g.vector.tensor_scalar(ap(o), src, bias, None, A.add)
-        add(q, fn, rd + [off], [o], 60 + (o[2] - o[1]) * GA * CY)
+            return g.vector.tensor_scalar(ap(o), src, bias, None, A.add) if bias else g.vector.tensor_copy(ap(o), src)
+        add("V", on_v, rd + [off], [o], (50, 0, o[2] - o[1]))
+        add("S", lambda g: g.scalar.activation(ap(o), ap(win).indirect(ap(off)), F.Identity, bias=bias), rd + [off], [o],
+            (65, 0, o[2] - o[1]))
+        either()
+
+    def gather_less(o, win, off, rd, b):
+        add("V", lambda g: g.vector.tensor_tensor(ap(o), ap(win).indirect(ap(off)), ap(b), A.subtract), rd + [off, b], [o],
+            (50, 0, o[2] - o[1]))
 
     def scatter(win, off, i, wr):
-        add("V", lambda g: g.vector.tensor_copy(ap(win).indirect(ap(off)), ap(i)), [off, i], wr, 50 + (i[2] - i[1]) * SCA * CY)
+        add("V", lambda g: g.vector.tensor_copy(ap(win).indirect(ap(off)), ap(i)), [off, i], wr, (50, 0, 0, i[2] - i[1]))
 
     def iota(o, pat, base, cm, wr=None):
         kw = {} if SCRATCH[o[0]][2] == I32 else dict(allow_small_or_imprecise_dtypes=True)
-        add("G", lambda g: g.iota(ap(o), pat, base, cm, **kw), [], wr or [o], 130 + 2 * (o[2] - o[1]) * CY)
+        add("G", lambda g: g.iota(ap(o), pat, base, cm, **kw), [], wr or [o], (130, 2 * (o[2] - o[1])))
 
     def sel(o, i, base, op, fill, pat=((-1, 128),), cm=1):
-        add("G", lambda g: g.affine_select(ap(o), ap(i), [list(x) for x in pat], op, fill, base, cm), [i], [o], 170 + 256 * CY)
+        add("G", lambda g: g.affine_select(ap(o), ap(i), [list(x) for x in pat], op, fill, base, cm), [i], [o], (170, 256))
 
     def mm(groups, first=True, last=True):
-        rd, wr, cost = [], [], 60.0
+        rd, wr, cyc = [], [], 0
+        (rd if first and last else wr).append("open" + groups[0][0][0])
         for o, terms in groups:
             wr.append(o)
             for l, r, st in terms:
                 rd += [l, r]
-                cost += max(64, o[2] - o[1]) * PC * (4 if SCRATCH[l[0]][2] == F32 else 1)
+                cyc += max(64, o[2] - o[1]) * (4 if SCRATCH[l[0]][2] == F32 else 1)
 
         def fn(g):
             ins = None
@@ -111,7 +139,7 @@ def build(T, send):
                     rhs = ap(r) if st == 1 else T[r[0]][:, r[1]:r[2]:st]
                     ins = g.tensor.matmul(ap(o), ap(l), rhs, first and k == 0, last and k == len(terms) - 1)
             return ins
-        add("P", fn, rd, wr, cost)
+        add("P", fn, rd, wr, (60, 0, 0, 0, cyc))
 
     def dma(q, pairs, rd, wr, nbytes, pri=0.0, **kw):
         def fn(g, sem):
@@ -119,7 +147,11 @@ def build(T, send):
             for o, i in pairs:
                 e.dma_start(o, i, **kw).then_inc(sem, 16)
             return 16 * len(pairs)
-        add(q, fn, rd, wr, (600 if q == "G" else 100) * len(pairs), kind="d", lat=1800 + nbytes / 250.0, pri=pri)
+        add(q, fn, rd, wr, ((600 if q == "G" else 100) * len(pairs),), kind="d", nbytes=nbytes, pri=pri)
+        if tag[0] == "a":
+            if loads:
+                ops[-1]["after"] = loads[-1]
+            loads.append(len(ops) - 1)
 
     def blk(name, k, n=128):
         return R(name, n * k, n * k + n)
@@ -128,7 +160,8 @@ def build(T, send):
         return [(R(z, 15 - i, 143 - i), R(src, a + i, b), 16) for i in range(16)]
 
     NT = ["ntA", "ntB", "ntC", "ntD"]
-    CW = ["cwA", "cwB"]
+    CW = ["cwA", "cwB", "cwZ"]
+    nt, cw = R("nt", 0, VZ), R("cw", 0, VZ)
     dma("Y", [(T.nxi[:], T.nx[:])], [], ["nxi"], 1 << 18, pri=1e5)
     dma("S", [(T.curi[:], T.cur[:])], [], ["curi"], 1 << 15, pri=1e5)
     dma("S", [(T.wti[:], T.wt[:])], [], ["wti"], 512, pri=1e5)
@@ -140,7 +173,7 @@ def build(T, send):
     act(R("nt", 5376, 6912), R("nt", 0, 1536), F.Copy, rd=["f0"], wr=["f4"])
     iota(R("pi", 0, 1), [[0, 1]], 0, 1)
     iota(R("ti"), [[1, 144]], 0, 0)
-    iota(R("nt", 6912, V), [[0, V - 6912]], 0, 0, ["f3"])
+    iota(R("nt", 6912, VZ), [[0, VZ - 6912]], 0, 0, ["f3"])
     cp(R("nhi"), R("nxi"))
     tt(R("nlo"), R("nxi"), R("nhi"), A.subtract)
     zr = ["f1", "f2", "f3", "f4"]
@@ -148,52 +181,61 @@ def build(T, send):
     dma("Y", [(T.nt[1:128:16, 0:V], T.nlo[:])], ["nlo"] + zr, ["ntB", "ntC", "ntD"], 1 << 17)
     dma("Y", [(T.cw[:, V // 2:V], T.cards[:, V // 2:V])], ["nlo"] + zr, ["cwB"], 1 << 20, pri=-1e5)
     cp(R("xo", 0, 64), R("curi"))
+    ms(R("cw", V, VZ), 0.0, ["cwZ"])
     ts(R("pi", 1, 2), R("pi", 0, 1), 15, None, A.bitwise_and)
     ts(R("pi", 2, 3), R("pi", 0, 1), 4, None, A.logical_shift_right)
     ts(R("pi", 3, 4), R("pi", 0, 1), 1, None, A.bitwise_and)
     ts(R("pi", 4, 5), R("pi", 0, 1), 3, None, A.bitwise_and)
     ts(R("pi", 5, 6), R("pi", 0, 1), 15, 2, A.bitwise_and, A.logical_shift_right)
     cp(R("pf", 0, 6), R("pi", 0, 6))
-    ic, gi, par, p3, qc, g16, lo2, sw, cc, r2, wf = (R("pf", k, k + 1) for k in range(1, 12))
+    ic, gi, par, p3, qc, g16, lo2, sw, cc, r2, wf, thr = (R("pf", k, k + 1) for k in range(1, 13))
     ts(g16, gi, 16.0, None, A.mult)
     ts(lo2, ic, 1.5, None, A.is_lt)
     ts(R("zs"), R("ti"), 15.0, g16, A.subtract, A.is_equal)
-    ts(R("zc"), R("zs"), lo2, None, A.mult)
+    scaled(R("zc"), R("zs"), lo2)
     cp(wf, R("wti"))
-    act(R("zw"), R("zs"), F.Identity, scale=wf)
+    scaled(R("zw"), R("zs"), wf)
     iota(R("di"), [[1, 128]], 0, -1)
     iota(R("tg"), [[16, 8], [0, 16]], 0, 0)
     iota(R("jj"), [[16, 32]], 0, 1)
-    iota(R("j8"), [[16, 32]], V, 1)
+    iota(R("j8", 0, 32), [[16, 32]], V + VZ, 1)
+    iota(R("j8", 32, 44), [[16, 12]], VZ, 1)
     iota(R("jm"), [[16, 32]], -1535, 1)
-    ms(R("cp", 0, S), 0.0)
-    zero = R("cp", 0, 128)
-    idp, idn, idf, bd = R("idp"), R("idn"), R("idf"), R("bd")
+    iota(R("cp", 0, S), [[0, S]], 0, 0)
+    zero, idp, idn, big, bd = R("zer"), R("idp"), R("idn"), R("big"), R("bd")
+    ms(zero, 0.0)
+    rows = ((-16, 8), (0, 16))
+    sel(big, zero, 0, A.not_equal, 16.0 * V)
+    ts(bd, R("tg"), g16, None, A.is_equal)
+    ts(thr, ic, 9.0, 0.5, A.not_equal, A.subtract)
     sel(idp, zero, 0, A.not_equal, 1.0)
     sel(idn, zero, 0, A.not_equal, -1.0)
+    sel(blk("sc1", 0), zero, -8, A.not_equal, 0.25, rows)
+    sel(blk("sc1", 1), blk("sc1", 0), -9, A.not_equal, -0.5, rows)
+    for i in range(8):
+        sel(blk("selt", i), blk("sc1", 1), -i, A.not_equal, 0.25, rows)
     sel(R("sa"), zero, 16, A.not_equal, 1.0)
     sel(R("sh"), R("sa"), -112, A.not_equal, 1.0)
-    act(idf, idp, F.Copy)
-    ts(bd, R("tg"), g16, None, A.is_equal)
-    for i in range(8):
-        sel(blk("selt", i), zero, -i, A.not_equal, 1.0, ((-16, 8), (0, 16)))
-    ts(R("tih"), R("ti", 0, 66), -0.5, None, A.add)
+    ts(R("tih"), R("ti", 0, 66), -64.5, None, A.add)
+    iota(R("til"), [[1, 64]], -64, 0)
     ts(sw, par, -2.0, 1.0, A.mult, A.add)
     ts(R("swf"), R("di"), sw, None, A.is_equal)
     ts(cc, gi, 4.0, p3, A.mult, A.add)
     ts(R("rs"), R("ti", 0, 32), cc, None, A.is_equal)
     ts(R("q4"), R("ti", 0, 4), qc, None, A.is_equal)
-    act(R("tib"), R("ti", 0, 128), F.Copy)
+    iota(R("tib"), [[64, 128]], V + 64, 0)
     ts(r2, ic, 2.0, 16384.0, A.is_equal, A.mult)
     tt(R("zq", 0, 143), R("zs", 0, 143), R("zs", 1, 144), A.add)
-    act(R("zp", 0, 143), R("zq", 0, 143), F.Identity, scale=r2)
+    scaled(R("zp", 0, 143), R("zq", 0, 143), r2)
     act(R("ua"), bd, F.Identity, scale=-1.0)
     sel(R("ub"), R("ua"), 0, A.is_ge, 0.0)
     sel(R("un"), R("ub"), 0, A.not_equal, -2048.0)
     for d in range(7):
         sel(blk("shd", d), R("sh"), d + 1, A.is_equal if d else A.is_ge, 0.0, ((-1, 8), (0, 16)), 0)
-    ms(R("one"), 1.0)
-    ms(R("sb", S, W), 0.0)
+    iota(R("one"), [[0, 32]], 1, 0)
+    iota(R("sb", S + 12, W), [[0, W - S - 12]], 0, 0)
+    if OPT["fuse"]:
+        move(R("z4"), R("zz", 0, L), -0.25)
 
     def xo(r, s, h=None):
         return blk("xo", 9 * r + s, 64) if h is None else blk("xo", 18 * r + 2 * s + h, 32)
@@ -204,94 +246,111 @@ def build(T, send):
     def zz(r, h):
         return blk("zz", 2 * r + h, 512)
 
-    def chase(r):
-        for s in range(1, 9):
-            b, tag[0], e = L * (s % 2), "c%d%d" % (r, s), P["ch"][r][s - 1]
-            if len(e) == 2:
-                for h in range(2):
-                    gather(e[h], R("gch", b + 512 * h, b + 512 * h + 512), R("nt", 0, V), xo(r, s - 1, h), NT)
-            else:
-                gather(e, R("gch", b, b + L), R("nt", 0, V), xo(r, s - 1), NT)
-            mm([(blk("pch", s - 1, 64), wrap("zc", "gch", b, b + L))])
-            cp(xo(r, s), blk("pch", s - 1, 64))
+    def halves(o, win, off, rd, bias=0.0):
+        n = 1 if tag[0][:2] in OPT["whole"].split() else 2
+        t = tag[0]
+        for h in range(n):
+            tag[0] = t + str(h)
+            gather(R(o[0], o[1] + L // n * h, o[1] + L // n * (h + 1)), win, R(off[0], off[1] + 64 // n * h, off[1] + 64 // n * (h + 1)),
+                   rd, bias)
+        tag[0] = t
+
+    def listed(r, s):
+        y, terms = blk("pch", s - 1, 64), wrap("zc", "gch", L * (s - 1), L * s)
+        if s == 1:
+            mm([(y, terms)])
+            cp(xo(r, s), y)
+            move(R("mn"), y, 7.0 * V)
+        else:
+            mm([(y, [(big, blk("mk", s - 1, 64), 1)] + terms)])
+            ts(xo(r, s), y, float(-V * (8 - s)), float(V), A.add, A.min)
+            tt(R("mn" if s < 8 else "um"), y, R("mn"), A.min)
+
+    def chase(r, steps):
+        raw = OPT["raw"] if r else 0
+        for s in steps:
+            tag[0] = "c%d%d" % (r, s)
+            halves(blk("gch", s - 1, L), nt, blk("xr", s - 1, 64) if 1 < s - 1 <= raw else xo(r, s - 1), NT)
+            if 1 < s <= raw:
+                mm([(blk("pch", s - 1, 64), wrap("zc", "gch", L * (s - 1), L * s))])
+                cp(blk("xr", s, 64), blk("pch", s - 1, 64))
+            elif s != raw + 1 or s == 1:
+                listed(r, s)
 
     def cards(r, steps):
         for s in steps:
-            for h in range(2):
-                tag[0] = "k%d%d%d" % (r, s, h)
-                gather(P["cg"][r][2 * s - 2 + h], cd(r, s, h), R("cw", 0, V), xo(r, s, h), CW, bias=0.25 * min(s, 8))
+            tag[0] = "k%d%d" % (r, s)
+            if OPT["fuse"] and (r, s) == (0, 1):
+                for h in range(2):
+                    gather_less(blk("dd", h, 512), cw, xo(r, s, h), CW, blk("z4", h, 512))
+            else:
+                halves(blk("cd", 9 * r + s - 1, L), cw, xo(r, s), CW, 0.25 * min(s, 8))
 
     def turns(r):
         tag[0] = "t%d" % r
-        gs = [(R("pm1", 128, 192), wrap("zw", "zz", L * r, L * r + L))]
-        for h in range(2):
-            gs.append((blk("pm1", 3 + h, 64), [(R("zw", 15 - i, 143 - i), blk("zz", 16 * r + 8 * h + i, 64), 1) for i in range(8)]))
-        mm(gs)
-        cp(R("ci"), R("pm1", 128, 320))
+        mm([(R("pm1", 128, 192), wrap("zw", "zz", L * r, L * r + L))])
+        cp(R("ci"), R("pm1", 128, 192))
         ts(R("cj"), R("ci"), 7, None, A.bitwise_and)
-        cp(R("cq"), R("cj", 64, 192))
-        for s in range(1, 8):
-            act(blk("pen", s), R("cq"), F.Relu, bias=32.0 * s, scale=-32.0)
-        for s in range(8):
-            ts(blk("eq", s, 64), R("cj", 0, 64), float(s), None, A.is_equal)
+        for s in range(2, 9):
+            ts(blk("mk", s - 1, 64), R("cj"), s - 1.0, (8 - s) / 16, A.is_lt, A.max)
+        for s in range(2, OPT["raw"] + 2 if r else 0):
+            tag[0] = "l%d%d" % (r, s)
+            listed(r, s)
 
     def cuts(r):
         g2, tag[0] = L * r, "u%d" % r
-        for s in range(8):
-            tt(blk("pr", s, 64), blk("eq", s, 64), blk("pch", s, 64), A.mult)
-            mm([(R("pm1", 0, 64), [(idf, blk("pr", s, 64), 1)])], s == 0, s == 7)
+        ts(R("uu"), R("um"), V - 1, None, A.bitwise_and)
         for a in range(4):
-            ts(blk("l4", a, 32), R("pm1", 0, 32), R("q4", a, a + 1), None, A.mult)
-        cp(R("uo"), R("pm1", 0, 64))
+            ts(blk("l4", a, 32), R("uu", 0, 32), float(V), R("q4", a, a + 1), A.add, A.mult)
+        cp(R("uo"), R("uu"))
         mm([(R("pm1", 64, 96), [(R("l4"), R("rs"), 1)])])
-        cp(R("ui"), R("pm1", 64, 96))
-        ts(R("uj", 0, 32), R("ui"), 6, None, A.logical_shift_right)
-        ts(R("uj", 32, 64), R("ui"), 63, None, A.bitwise_and)
-        cp(R("hl"), R("uj"))
-
-        def reveal():
-            tag[0] = "v%d" % r
-            for h in range(2):
-                gather(P["g2"][r][h], blk("g2", 2 * r + h, AC), R("nt", 0, V), blk("uo", h, 32), NT)
-            mm([(R("pm2", 0, 64), wrap("zc", "g2", g2, g2 + L))])
-            cp(xo(r, 9), R("pm2", 0, 64))
-
-        early = P["ev"][r] == "Y"
-        if early:
-            reveal()
+        move(R("hl", 0, 32), R("pm1", 64, 96), 32.5)
+        tt(R("hl", 32, 64), R("pm1", 64, 96), R("hl", 0, 32), A.subtract)
+        mm([(R("pm1", 96, 128), [(R("swf"), blk("l4", a, 32), 1) for a in range(4)])], last=False)
+        tag[0] = "v%d" % r
+        gather(blk("g2", 2 * r + 1, AC), nt, blk("uo", 1, 32), NT)
         for k in range(2):
-            bank, h0, step = ("phb", "pm2")[k], 128 * k, P["oh"][r][4 * k] == "S"
-            w, tag[0] = 65 if step else 64, "h%d%d" % (r, k)
+            bank, h0, step = ("phb", "pm2")[k], 128 * k, OPT["step"][2 * r + k] == "S"
+            w = 65 if step else 64
             for gq in range(4 * k, 4 * k + 4):
+                tag[0] = "h%d%d" % (r, gq)
                 for c in range(4 * gq, 4 * gq + 4):
                     ts(blk("ohh", c), R("tib"), R("hl", c, c + 1), None, A.is_equal)
+                    lo, oh = R("hl", 32 + c, 33 + c), R("ohl", 66 * c, 66 * c + w)
                     if step:
-                        act(R("ohl", 66 * c, 66 * c + w), R("tih", 0, w), F.Sign, bias=R("hl", 32 + c, 33 + c), scale=-1.0)
+                        ts(oh, R("tih", 0, w), lo, 2.0, A.is_lt, A.mult)
+                        act(oh, R("tih", 0, w), F.Sign, bias=lo, scale=-1.0)
+                        either()
                     else:
-                        ts(R("ohl", 66 * c, 66 * c + w), R("tib", 0, w), R("hl", 32 + c, 33 + c), None, A.is_equal)
+                        ts(oh, R("til"), lo, None, A.is_equal)
                 a = h0 + w * (gq % 4)
                 mm([(R(bank, a, a + w), [(blk("ohh", c), R("ohl", 66 * c, 66 * c + w), 1) for c in range(4 * gq, 4 * gq + 4)])])
-            f0 = 260 * k
+            f0, tag[0] = 260 * k, "m%d%d" % (r, k)
             if step:
-                act(R("cs", f0, f0 + 260), R(bank, h0, h0 + 260), F.Identity, bias=3.0)
+                move(R("cs", f0, f0 + 260), R(bank, h0, h0 + 260), 3.0)
                 tt(R("fl", f0, f0 + 259), R(bank, h0, h0 + 259), R("cs", f0 + 1, f0 + 260), A.is_gt)
             else:
+                ts(R("fl", f0, f0 + 256), R(bank, h0, h0 + 256), 1.5, None, A.is_gt)
                 act(R("fl", f0, f0 + 256), R(bank, h0, h0 + 256), F.Relu, bias=-1.0)
+                either()
             dma("Y", [(T.nt[64 * k + 16 * j + 2:64 * k + 16 * j + 3, 0:V], T.fl[:, f0 + w * j:f0 + w * j + 64]) for j in range(4)],
                 [R("fl", f0, f0 + 260)], [NT[2 + k]], 1 << 16)
-        if early:
-            tag[0] = "x%d" % r
-            gather("S", R("g3"), R("nt", 0, V), R("uo", 0, 32), NT)
-        else:
-            reveal()
-        tag[0], (m0, m1) = "x%d" % r, ("g3", 0) if early else ("g2", g2)
-        mm([(R("pm1", 96, 128), [(R("swf"), blk("l4", a, 32), 1) for a in range(4)]
-             + [(R("zp", 14 - (i & 14), 142 - (i & 14)), R(m0, m1 + i, m1 + AC), 16) for i in range(16)])])
-        tt(R("t1"), R("j8"), R("pm1", 96, 128), A.min)
-        cp(R("o1"), R("t1"))
+        tag[0] = "v%d" % r
+        gather(blk("g2", 2 * r, AC), nt, blk("uo", 0, 32), NT)
+        mm([(R("pm2", 0, 64), wrap("zc", "g2", g2, g2 + L))])
+        cp(xo(r, 9), R("pm2", 0, 64))
+        tag[0] = "x%d" % r
+        mm([(R("pm1", 96, 128), [(R("zp", 14 - (i & 14), 142 - (i & 14)), R("g2", g2 + i, g2 + AC), 16) for i in range(16)])], False)
         if r == 0:
-            ts(R("cut"), R("pm1", 96, 128), float(V), None, A.is_lt)
-        scatter(R("nt"), R("o1"), R("g2", g2, g2 + AC), NT)
+            ts(R("cut"), R("pm1", 96, 128), 2.0 * V, None, A.is_lt)
+        tt(R("t1"), R("j8", 0, 32), R("pm1", 96, 128), A.min)
+        ts(R("o1"), R("t1"), -float(V), None, A.add)
+        if r == 0:
+            scatter(R("nt"), R("o1"), R("g2", 0, AC), NT)
+        else:
+            mm([(R("phb"), [(R("zc", 15, 143), R("g2", L, L + AC), 1)])])
+            move(R("vf"), R("phb"))
+            scatter(R("nf"), R("o1"), R("vf"), ["nf"])
 
     def deal():
         tag[0] = "d0"
@@ -300,71 +359,87 @@ def build(T, send):
         mm([(R("pm2", 64, 96), [(bd, R("s1"), 1), (R("un"), R("cut"), 1)]), (R("pm2", 96, 97), [(bd, R("s1", 31, 32), 1)])])
         tt(R("t2"), R("jm"), R("pm2", 64, 96), A.min)
         ts(R("o2"), R("t2"), 2047.0, None, A.add)
-        ts(R("cnt", 0, 1), R("pm2", 96, 97), float(S), None, A.min)
-        cp(R("sb", S, S + 1), R("cnt", 0, 1))
+        far, top, aim = R("sb", S, S + 12), R("pm2", 100, 112), R("pm2", 112, 124)
+        ts(R("cnt"), R("pm2", 96, 97), g16, None, A.add)
+        ts(far, R("jj", 0, 12), R("cnt"), 4.0 * V, A.is_ge, A.mult)
         scatter(R("cp"), R("o2"), R("g2", 0, AC), ["cp"])
-        mm([(R("pm2", 100, 112), wrap("zc", "cp", 0, S))])
-        cp(R("to"), R("pm2", 100, 112))
-        cp(R("tf"), R("pm2", 100, 112))
-        gather("S", R("sb", 0, S), R("cw", 0, V), R("to"), CW)
-        add("G", send, ["sb"], ["land"], 1000, kind="r", lat=4500)
+        mm([(top, wrap("zc", "cp", 0, S))])
+        cp(R("to"), top)
+        gather(R("sb", 0, S), cw, R("to"), CW)
+        add("G", send, ["sb"], ["land"], (1000,), kind="r")
         tag[0] = "d1"
-        mm([(R("phb", 0, W), [(blk("shd", d), blk("land", d, W), 1) for d in range(7)])])
-        act(R("ar"), R("phb", 0, W), F.Copy)
-        ts(R("cnt", 1, 2), R("ar", S, S + 1), R("cnt", 0, 1), g16, A.min, A.add)
-        ts(R("t3"), R("jj", 0, 12), R("cnt", 1, 2), 16384.0, A.is_ge, A.mult)
-        tt(R("t4"), R("t3"), R("tf"), A.add)
-        tt(R("t5"), R("t4"), R("j8", 0, 12), A.min)
+        mm([(aim, wrap("zc", "cp", 0, S) + [(idp, far, 1)])], last=False)
+        mm([(aim, [(blk("shd", d), R("land", W * d + S, W * d + S + 12), 1) for d in range(7)])], False)
+        mm([(R("phb", 0, S), [(blk("shd", d), R("land", W * d, W * d + S), 1) for d in range(7)])])
+        move(R("ar"), R("phb", 0, S))
+        tt(R("t5"), R("j8", 32, 44), aim, A.min)
         cp(R("o3"), R("t5"))
-        scatter(R("cw"), R("o3"), R("ar", 0, S), CW)
+        scatter(R("cw"), R("o3"), R("ar"), CW)
+        tag[0] = "n"
+        dma("G", [(T.nf[0:128:16, 0:V], T.nt[0:128:16, 0:V])], NT[:1] + ["land"], ["nf"], 1 << 18)
+        dma("G", [(T.nf[0:128:16, 0:V], T.nt[1:128:16, 0:V])], NT[1:2], ["nf"], 1 << 19, accum_op=A.add, max_dma_last_dim=4096)
 
     def walk(r):
-        for h in range(2):
-            pd, tag[0] = R("pd%d" % h), "w%d0%d" % (r, h)
-            mm([(pd, [(idp, cd(r, 1, h), 1), (idn, zz(r, h), 1)])])
-            if P["d1"][r] == "S":
-                act(blk("dd", h, 512), pd, F.Copy)
+        fused = OPT["fuse"] and r == 0
+        parts, a, banks = [], 0, PSUM[:4]
+        for n in OPT["parts"][r]:
+            f, banks = banks[0], banks[1:]
+            if n > 4:
+                pd, banks = R(banks[0], 0, 64 * n), banks[1:]
             else:
-                cp(blk("dd", h, 512), pd)
+                pd = R(f, 256, 256 + 64 * n)
+            parts.append((a, n, f, pd))
+            a += 64 * n
+
+        def cut(name, k, a, n):
+            return R(name, L * k + a, L * k + a + 64 * n)
+
+        for h, (a, n, pf, pd) in enumerate([] if fused else parts):
+            tag[0] = "w%d0%d" % (r, h)
+            mm([(pd, [(idp, cut("cd", 9 * r, a, n), 1), (idn, cut("zz", r, a, n), 1)])])
+            move(cut("dd", 0, a, n), pd)
         for s in range(1, 9):
-            for h in range(2):
-                pd, pf, tag[0] = R("pd%d" % h), "pf%d" % h, "w%d%d%d" % (r, s, h)
-                d, b, rr, fs = blk("dd", h, 512), blk("bb", h, 512), blk("rr", h, 512), blk("fs", h, 64)
-                on_s = P["bs"][r][2 * s - 2 + h] == "S"
-                if on_s:
-                    act(b, d, F.Sign, bias=-0.5)
-                else:
-                    ts(b, d, 0.5, None, A.is_gt)
-                pen = [(idn, blk("pen", 2 * s - 2 + h, 64), 1)] if s > 1 else []
-                mm([(R(pf, 0, 64), pen + [(R("zs", 15 - i, 143 - i), blk("bb", 8 * h + i, 64), 1) for i in range(8)])])
-                ts(fs, R(pf, 0, 64), 1.0 if on_s else 8.5, 0.5, A.is_lt, A.max)
-                mm([(blk(pf, i, 64), [(blk("selt", i), fs, 1)]) for i in range(8)])
-                mm([(pd, [(idp, cd(r, s + 1, h), 1), (idn, cd(r, s, h), 1)])])
-                tt(rr, d, R(pf), A.mult)
+            for h, (a, n, pf, pd) in enumerate(parts):
+                tag[0] = "b%d%d%d" % (r, s, h)
+                d, b, rr, fs = cut("dd", 0, a, n), cut("bb", 0, a, n), cut("rr", 0, a, n), blk("fs", h, 64)
+                ts(b, d, 0.5, 0.5, A.is_gt, A.subtract)
+                act(b, d, F.Sign, bias=-0.5)
+                either()
+                mm([(R(pf, 0, 64), [(R("zs", 15 - i, 143 - i), cut("bb", 0, a + 64 * i, 1), 1) for i in range(n)])])
+                tag[0] = "f%d%d%d" % (r, s, h)
+                ts(fs, R(pf, 0, 64), thr, 2.0, A.is_lt, A.mult)
+                act(fs, R(pf, 0, 64), F.Sign, bias=thr, scale=-1.0)
+                either()
+                tag[0] = "w%d%d%d" % (r, s, h)
+                old = [(idn, d, 1), (idn, cut("zz", r, a, n), 1)] if fused and s == 1 else [(idn, cut("cd", 9 * r + s - 1, a, n), 1)]
+                mm([(pd, old + [(idp, cut("cd", 9 * r + s, a, n), 1)])])
+                mm([(blk(pf, i, 64), [(blk("selt", i), fs, 1)]) for i in range(n)])
+                tt(rr, d, R(pf, 0, 64 * n), A.mult)
                 if s < 8:
                     tt(d, rr, pd, A.add)
                 else:
-                    tt(blk("db", h, 512), rr, pd, A.add)
-                    act(zz(r + 1, h), blk("db", h, 512), F.Abs)
-                    if r == 1:
-                        dma("Y", [(T.yz[:, 512 * h:512 * h + 512], ap(zz(2, h)))], [zz(2, h)], ["yz%d" % h], 1 << 17)
+                    tt(cut("db", 0, a, n), rr, pd, A.add)
+                    act(cut("zz", r + 1, a, n), cut("db", 0, a, n), F.Abs)
+                    if r == 1 and (a + 64 * n) % 512 == 0:
+                        k = a // 512
+                        dma("Y", [(T.yz[:, 512 * k:512 * k + 512], ap(zz(2, k)))], [zz(2, k)], ["yz%d" % k], 1 << 17)
 
     turns(0)
-    chase(0)
+    chase(0, range(1, 9))
     cards(0, range(1, 9))
     cuts(0)
     cards(0, [9])
     deal()
-    chase(1)
+    chase(1, range(1, OPT["raw"] + 2))
     walk(0)
     turns(1)
+    chase(1, range(OPT["raw"] + 2, 9))
     cards(1, range(1, 9))
     cuts(1)
     cards(1, [9])
     tag[0] = "y"
-    dma("G", [(T.yn[:], T.nt[0:128:16, 0:V])], NT, ["yn"], 1 << 18)
+    dma("Y", [(T.yn[:], T.nf[0:128:16, 0:V])], ["nf"], ["yn"], 1 << 18)
     dma("G", [(T.yc[:], T.g2[0:128:16, L:2 * L])], [R("g2", L, 2 * L)], ["yc"], 1 << 15)
-    dma("G", [(T.yn[:], T.nt[1:128:16, 0:V])], NT, ["yn"], 1 << 19, accum_op=A.add, max_dma_last_dim=4096)
     dma("G", [(T.yc[:], T.g2[1:128:16, L:2 * L])], [R("g2", L, 2 * L)], ["yc"], 1 << 16, accum_op=A.add, max_dma_last_dim=4096)
     walk(1)
     return ops
@@ -385,65 +460,154 @@ def depend(ops):
                 if kind == "w":
                     h[:] = [e for e in h if not (a <= e[2] and e[3] <= b)]
                 h.append((n, kind, a, b))
-        deps.append(ds)
+        deps.append(sorted(ds))
     return deps
 
 
-def chains(ops, deps):
-    n = len(ops)
+def lengths(ops, tm):
+    cost = [{q: tm["call"][q] + max(64, s[1]) * tm["cy"] if q in "VS" and s[1] else
+             (tm["call"][q] if q == "P" else s[0]) + (s[1] + s[2] * tm["ga"] + s[3] * tm["sc"]) * tm["cy"] + s[4] * tm["pc"]
+             for q, (_, s) in o["on"].items()} for o in ops]
+    lat = [tm["dma"] + o["nbytes"] / tm["rate"] if o["kind"] == "d" else tm["send"] if o["kind"] == "r" else 0.0 for o in ops]
+    return cost, lat
+
+
+def place(ops, deps, tm, urge, lean):
+    n, wake = len(ops), tm["wake"]
+    cost, lat = lengths(ops, tm)
+    deps = [d + [o["after"]] if "after" in o else d for d, o in zip(deps, ops)]
     succ, tail = [[] for _ in range(n)], [0.0] * n
     for k in range(n):
         for m in deps[k]:
             succ[m].append(k)
     for k in range(n - 1, -1, -1):
-        tail[k] = ops[k]["cost"] + ops[k]["lat"] + WAKE + max([tail[j] for j in succ[k]] + [0.0])
-    return succ, tail
-
-
-def dispatch(ops, deps, succ, tail, urge):
-    n = len(ops)
-    prio = [tail[k] + ops[k]["pri"] + urge.get(ops[k]["tag"], 0) for k in range(n)]
-    slack, idle = max(0, urge.get("sl", 0) / 10), urge.get("sm", 0) / 300
-    left, at, free, bk, order = [len(d) for d in deps], [0.0] * n, {q: 0.0 for q in "VSPGY"}, {}, []
-    ready = {q: [k for k in range(n) if left[k] == 0 and ops[k]["q"] == q] for q in "VSPGY"}
-    while len(order) < n:
-        bt = None
-        for q in "VSPGY":
-            st = []
-            for k in ready[q]:
-                t = max(at[k], free[q])
-                for b in ops[k]["banks"]:
-                    e = bk.get(b)
-                    if e and e[1] != q and e[0] + WAKE > t:
-                        t = e[0] + WAKE
-                st.append((t, k))
-            if st and (bt is None or min(st)[0] < bt[0]):
-                bt = (min(st)[0], q, st)
-        t0, q, st = bt
-        t, k = max(((t, k) for t, k in st if t <= t0 + slack), key=lambda x: prio[x[1]] - idle * (x[0] - t0))
-        ready[q].remove(k)
-        order.append(k)
-        free[q] = t + ops[k]["cost"]
-        for b in ops[k]["banks"]:
-            bk[b] = (free[q], q)
+        tail[k] = min(cost[k].values()) + lat[k] + wake + max([tail[j] for j in succ[k]] + [0.0])
+    for k, o in enumerate(ops):
+        t = ("w" if o["tag"][0] in "bf" else o["tag"][0]) + o["tag"][1:2]
+        a, b = urge.get(t, (0, 0))
+        tail[k] += o["pri"] + 100 * (a + b * int(o["tag"][2:3] or 0) - urge.get("H" + t, (0,))[0] * int(o["tag"][3:4] or 0))
+    left, busy, start, end, eng = [len(d) for d in deps], {}, [0.0] * n, [0.0] * n, [None] * n
+    ready = [k for k in range(n) if not left[k]]
+    while ready:
+        k = max(ready, key=lambda x: (tail[x], -x))
+        ready.remove(k)
+        best = None
+        for q, c in cost[k].items():
+            t, again = max([end[m] + (0.0 if m == ops[k].get("after") else lat[m] + (tm["same"] if eng[m] == q else wake))
+                            for m in deps[k]] + [0.0]), True
+            while again:
+                again = False
+                for key in [q] + ops[k]["banks"]:
+                    for a, b, q2 in busy.get(key, ()):
+                        pad = 0.0 if key == q else wake
+                        if a - pad < t + c and b + pad > t and (key == q or q2 != q):
+                            t, again = b + pad, True
+            v = t + c - (100 * lean.get(ops[k]["tag"][:2], 0) if q == "V" else 0)
+            if best is None or v < best[0]:
+                best = v, t, q
+        start[k], eng[k] = best[1:]
+        end[k] = start[k] + cost[k][eng[k]]
+        for key in [eng[k]] + ops[k]["banks"]:
+            busy[key] = sorted(busy.get(key, []) + [(start[k], end[k], eng[k])])
         for j in succ[k]:
-            at[j] = max(at[j], free[q] + ops[k]["lat"] + WAKE)
             left[j] -= 1
-            if left[j] == 0:
-                ready[ops[j]["q"]].append(j)
-    return order
+            if not left[j]:
+                ready.append(j)
+    return sorted(range(n), key=lambda x: (start[x], x)), eng
 
 
-def emit(g, T, ops, order, deps):
+def refine(ops, deps, tm, order, eng, tries, heat, seed=1):
+    n, wake, near = len(ops), tm["wake"], tm["wake"] - tm["same"]
+    cost, lat = lengths(ops, tm)
+    above = []
+    for k in range(n):
+        above.append(set(deps[k]).union(*[above[m] for m in deps[k]]))
+    need = [[m for m in deps[k] if not any(m in above[j] for j in deps[k])] for k in range(n)]
+    succ, prec = [[] for _ in range(n)], [d + [o["after"]] if "after" in o else d for d, o in zip(need, ops)]
+    for k in range(n):
+        for m in prec[k]:
+            succ[m].append(k)
+    banks, flex, rnd = [o["banks"] for o in ops], [k for k in range(n) if len(cost[k]) > 1], [seed]
+
+    def pick(m):
+        rnd[0] = (rnd[0] * 1103515245 + 12345) % 2147483648
+        return (rnd[0] >> 8) % m
+
+    def run(order, eng, first, marks, end, why):
+        i0 = first // 32
+        held, marks, end, why = dict(marks[i0]), marks[:i0], end[:], why[:]
+        for i in range(32 * i0, n):
+            if i % 32 == 0:
+                marks.append(dict(held))
+            k = order[i]
+            q = eng[k]
+            t, _, w = held[q]
+            for m in need[k]:
+                e = end[m] - near if eng[m] == q else end[m]
+                if e > t:
+                    t, w = e, m
+            for b in banks[k]:
+                e = held[b]
+                if e[1] != q and e[0] + wake > t:
+                    t, w = e[0] + wake, e[2]
+            t += cost[k][q]
+            e = held[q] = (t, q, k)
+            for b in banks[k]:
+                held[b] = e
+            end[k], why[k] = t + lat[k] + wake, w
+        return max(end), marks, end, why
+
+    now = run(order, eng, 0, [{x: (0.0, x, None) for x in list("VSPGY") + PSUM}], [0.0] * n, [None] * n)
+    best, fresh = (now[0], order, eng), True
+    for it in range(tries):
+        if fresh:
+            k, chain, fresh, pos = now[2].index(now[0]), [], False, {x: i for i, x in enumerate(order)}
+            while now[3][k] is not None:
+                chain.append((now[3][k], k))
+                k = now[3][k]
+            held_up = [p for p in chain if p[0] not in need[p[1]]]
+            loose = [p[1] for p in chain if len(cost[p[1]]) > 1] or flex
+        o2, e2, kind, far = order, eng, pick(20), (0, 0, 0, 2, 5, 12, 30)[pick(7)]
+        if kind < 3:
+            k = flex[pick(len(flex))] if kind == 0 else loose[pick(len(loose))]
+            e2, a = eng[:], pos[k]
+            e2[k] = "V" if eng[k] == "S" else "S"
+        else:
+            x, y = held_up[pick(len(held_up))]
+            up = kind < 12
+            a, b = (max(0, pos[x] - far), pos[y]) if up else (pos[x], min(n - 1, pos[y] + far))
+            seg, mv = order[a:b + 1], {y if up else x}
+            for j in (seg[::-1] if up else seg):
+                if any(m in mv for m in (succ if up else prec)[j]):
+                    mv.add(j)
+            if (x if up else y) in mv:
+                continue
+            o2 = order[:a] + [j for j in seg if (j in mv) == up] + [j for j in seg if (j in mv) != up] + order[b + 1:]
+        new = run(o2, e2, a, *now[1:])
+        if new[0] <= now[0] + heat * (1 - it / tries) * pick(1000) / 1000:
+            order, eng, now, fresh = o2, e2, new, True
+            if new[0] < best[0]:
+                best = new[0], o2, e2
+    return best[1:]
+
+
+def plan(ops):
+    if not PLAN:
+        deps = depend(ops)
+        PLAN["p"] = refine(ops, deps, TIME, *place(ops, deps, TIME, URGE, LEAN), *TRIES) + (deps,)
+    return PLAN["p"]
+
+
+def emit(g, T, ops, order, on, deps):
     eng = {"V": g.vector, "S": g.scalar, "P": g.tensor, "G": g, "Y": g.sync}
     count, know, token, last, pos = {}, {q: {} for q in eng}, {}, {}, {k: i for i, k in enumerate(order)}
     nd = 0
     for k in order:
-        o = ops[k]
-        q = o["q"]
+        o, q = ops[k], on[k]
+        fn = o["on"][q][0]
         need = list(deps[k])
         for b in o["banks"]:
-            if b in last and ops[last[b]]["q"] != q:
+            if b in last and on[last[b]] != q:
                 need.append(last[b])
             last[b] = k
         for m in sorted(need, key=lambda x: -pos[x]):
@@ -454,26 +618,23 @@ def emit(g, T, ops, order, deps):
                     know[q][s2] = max(know[q].get(s2, 0), seen[s2])
         if o["kind"] == "c":
             s = "q" + q
-            o["fn"](g).then_inc(T.sem[s], 1)
+            fn(g).then_inc(T.sem[s], 1)
             v = count.get(s, 0) + 1
         elif o["kind"] == "d":
             s = "d%d" % nd
             nd += 1
-            v = o["fn"](g, T.sem[s])
+            v = fn(g, T.sem[s])
         else:
             s = "arr"
-            v = count["sent"] = o["fn"](g)
+            v = count["sent"] = fn(g)
         count[s] = v
         token[k] = (s, v, dict(know[q], **{s: v}))
     for s in count:
         g.sync.wait_ge(T.sem[s], count[s])
 
 
-def rank_program(g, core, T, topo):
-    rank = T.rank_of(core)
-    if rank is None:
-        return
-    n = len(T.cores)
+def sender(core, T, topo):
+    rank, n = T.rank_of(core), len(T.cores)
 
     def send(g):
         peers = [T.cores[(rank + 1 + d) % n] for d in range(n - 1)]
@@ -487,11 +648,11 @@ def rank_program(g, core, T, topo):
                                          remote_sem=T.sem.arr, src=T.sb[:], dst=T.land[:, W * d:W * d + W]))
         g.remote_dma_fused(trs, local_sem=T.sem.sent)
         return 2 * len(peers)
+    return send
 
-    ops = build(T, send)
-    if not ORDER:
-        deps = depend(ops)
-        succ, tail = chains(ops, deps)
-        urge = {x.split(":")[0]: 100 * int(x.split(":")[1]) for x in URGE.split()}
-        ORDER["o"] = (dispatch(ops, deps, succ, tail, urge), deps)
-    emit(g, T, ops, *ORDER["o"])
+
+def rank_program(g, core, T, topo):
+    if T.rank_of(core) is None:
+        return
+    ops = build(T, sender(core, T, topo))
+    emit(g, T, ops, *plan(ops))

@@ -1,42 +1,42 @@
 from concourse.bass import DstId, RemoteDMATransfer
 from concourse.mybir import AluOpType as A, ActivationFunctionType as F
 
-V, L, AC, S, W = 8192, 1024, 512, 192, 208
+V, L, AC, S, W, Q = 8192, 1024, 512, 192, 208, 256
 VZ = V + 16
 BF, F32, I32, U16, F16 = "bfloat16", "float32", "int32", "uint16", "float16"
 SCRATCH = {}
 for _dt, _bufs in (
-        (BF, dict(cw=VZ + S + 128, nt=VZ + AC + 128, nhi=512, nlo=512, zz=3 * L, gch=8 * L, g2=2 * L, db=L, bb=L, fs=256,
-                  mk=512, hl=64, ohh=32 * 128, ohl=32 * 66, fl=520, cut=32, s1=32, cp=L + 128, sb=W, land=7 * W, ar=S,
-                  tib=128, tih=66, til=64, zs=144, zc=144, zw=144, zq=144, zp=144, idp=128, idn=128, big=128, bd=128, selt=1024,
-                  zer=128, sc1=256, ua=128, ub=128, un=128, sa=128, sh=128, shd=7 * 128, one=32)),
+        (BF, dict(cw=VZ + S + 128, nt=VZ + AC + 128, nhi=512, nlo=512, zz=3 * L, gch=8 * L, g2=2 * L, g3=AC, db=L, bb=L, fs=256,
+                  pen=1024, mk=512, hl=64, ohh=32 * 128, ohl=32 * 66, fl=576, cut=32, s1=32, g4=Q, cp=AC + 128, sb=W, land=7 * W, ar=S,
+                  tib=128, tih=66, zs=144, zc=144, zw=144, zq=144, zp=144, idp=128, idn=128, big=128, bd=128, selt=512,
+                  zer=128, sc1=256, zd=144, id2=256, be=256, ue=256, ua=128, ub=128, uc=128, un=128, sa=128, sh=128, shd=7 * 128, one=32)),
         (F16, dict(cd=18 * L, dd=L, z4=L)),
-        (I32, dict(nxi=512, curi=64, wti=1, rr=L, ci=64, cj=64, um=64, uu=64, pi=8)),
-        (U16, dict(xo=19 * 64, xr=8 * 64, uo=64, o1=32, o2=32, o3=12, to=12)),
-        (F32, dict(nf=VZ + AC + 128, vf=AC, mn=64, l4=128, cs=520, t1=32, t2=32, cnt=1, t5=12, pf=16, ti=144, di=128,
-                   tg=128, jj=32, j8=44, jm=32, swf=128, q4=4, rs=32))):
+        (I32, dict(nxi=512, curi=64, wti=1, rr=L, ci=64, cj=64, cq=512, um=64, uu=64, pi=8)),
+        (U16, dict(xo=19 * 64, xr=8 * 64, uo=64, o1=32, o2=16, o3=12, to=12)),
+        (F32, dict(nf=VZ + AC + 128, vf=AC, mf=512, uf=32, mn=64, l4=128, cs=576, t1=32, t2=16, cnt=1, t5=12, pf=16, ti=144,
+                   di=128, tg=128, jj=32, j8=44, jm=16, swf=128, q4=4, rs=32))):
     for _k in _bufs:
         SCRATCH[_k] = ("sbuf", [128, _bufs[_k]], _dt)
-PSUM = ["pd0", "pd1", "pf0", "pf1", "pch", "pm1", "pm2", "phb"]
+PSUM = ["pw0", "pw1", "pw2", "pw3", "pch", "pm1", "pm2", "phb"]
 for _k in PSUM:
     SCRATCH[_k] = ("psum", [128, 512], F32)
-SEMAPHORES = ["qV", "qS", "qP", "qG", "arr", "sent"] + ["d%d" % i for i in range(24)]
+SEMAPHORES = ["qV", "qS", "qP", "qG", "arr", "sent"] + ["d%d" % i for i in range(32)]
 
-TIME = dict(cy=0.85, pc=0.43, ga=1.45, sc=3.2, wake=220.0, same=100.0, dma=1100.0, rate=430.0, send=4500.0,
-            call=dict(V=5.0, S=20.0, P=35.0))
+OPT = dict(raw=5, pen=2, early="NY")
+TIMES = [dict(cy=1.00, pc=0.46, ga=1.9, sc=4.2, wake=235.0, same=100.0, dma=1150.0, rate=480.0, send=4300.0, call=dict(V=3.0, S=15.0, P=35.0)),
+         dict(cy=0.95, pc=0.46, ga=1.2, sc=2.5, wake=176.0, same=160.0, dma=1330.0, rate=570.0, send=5900.0, call=dict(V=0.0, S=15.0, P=41.0)),
+         dict(cy=0.83, pc=0.30, ga=1.5, sc=2.4, wake=286.0, same=55.0, dma=1300.0, rate=530.0, send=3400.0, call=dict(V=0.0, S=15.0, P=27.0))]
+URGE = dict(t0=1000, c0=1000, u0=1000, h0=1000, m0=1000, v0=1000, x0=1010, d0=1000, d1=1000, k0=20,
+            c1=300, t1=500, l1=300, u1=300, v1=300, k1=10)
+STAGGER = 5
+LEAN = dict(a=-20, c0=5, k0=-90, c1=-90, k1=-90, v0=-90, v1=-90, b0=10, f0=5, f1=5, h0=-2, h1=-10, m1=-5, w1=-5, x1=-10)
+TRIES = ((125000, 100.0, 3), (120000, 100.0, 4))
 PLAN = {}
-OPT = dict(raw=3, fuse=0, whole="c1", step="SSSS", parts=((4, 4, 4, 4), (4, 4, 4, 4)))
-URGE = {"Hw0": [6, 0], "Hw1": [5, 0], "a": [323, 0], "c0": [810, 81], "c1": [-2, 0], "d0": [309, 0], "d1": [-20, 0], "h0": [-12, -6],
-        "h1": [-1, 0], "k0": [-10, 1], "k1": [-5, -1], "l1": [255, -13], "m0": [-273, 0], "m1": [4, 0], "n": [120, 0], "t0": [-284, 0],
-        "t1": [306, 0], "u0": [-34, 0], "u1": [21, 0], "v0": [102, 0], "v1": [1125, 0], "w0": [-3, -1], "w1": [-6, 0], "x0": [-249, 0],
-        "x1": [311, 0], "y": [-469, 0]}
-LEAN = {"a": -90, "b0": 2, "b1": 0, "c0": 5, "c1": -5, "d0": -90, "d1": 2, "f0": -2, "f1": 10, "h0": -20, "h1": -20, "k0": -10, "k1": 0,
-        "m0": -90, "m1": -2, "u0": 5, "u1": -20, "v0": -90, "v1": -20, "w0": 2, "w1": 5, "x1": -20}
-TRIES = (100000, 300.0)
 
 
 def build(T, send):
     ops, tag, loads = [], ["a"], []
+    raw, pens = OPT["raw"], range(2, OPT["pen"] + 1)
 
     def R(name, a=0, b=None):
         return (name, a, (SCRATCH[name][1][1] if name in SCRATCH else 1) if b is None else b)
@@ -55,7 +55,7 @@ def build(T, send):
         return T[r[0]][:, r[1]:r[2]]
 
     def vc(i, f=1.0):
-        return 55, max(8, (i[2] - i[1]) * f)
+        return 0, max(8, (i[2] - i[1]) * f)
 
     def two(*rs):
         return 0.5 if all(SCRATCH[r[0]][2] in (BF, F16, U16) for r in rs) else 1.0
@@ -85,7 +85,7 @@ def build(T, send):
 
     def act(o, i, func, bias=0.0, scale=1.0, rd=None, wr=None):
         add("S", lambda g: g.scalar.activation(ap(o), ap(i), func, bias=sval(bias), scale=sval(scale)),
-            (rd or [i]) + cols(bias) + cols(scale), wr or [o], (65, i[2] - i[1]))
+            (rd or [i]) + cols(bias) + cols(scale), wr or [o], vc(i))
 
     def move(o, i, bias=0.0):
         if bias:
@@ -139,7 +139,7 @@ def build(T, send):
                     rhs = ap(r) if st == 1 else T[r[0]][:, r[1]:r[2]:st]
                     ins = g.tensor.matmul(ap(o), ap(l), rhs, first and k == 0, last and k == len(terms) - 1)
             return ins
-        add("P", fn, rd, wr, (60, 0, 0, 0, cyc))
+        add("P", fn, rd, wr, (0, 0, 0, 0, cyc))
 
     def dma(q, pairs, rd, wr, nbytes, pri=0.0, **kw):
         def fn(g, sem):
@@ -159,7 +159,10 @@ def build(T, send):
     def wrap(z, src, a, b):
         return [(R(z, 15 - i, 143 - i), R(src, a + i, b), 16) for i in range(16)]
 
-    NT = ["ntA", "ntB", "ntC", "ntD"]
+    def fold(z, src, k):
+        return [(R(z, 15 - i, 143 - i), blk(src, 4 * k + i, 64), 1) for i in range(4)]
+
+    NT = ["ntA", "ntB"] + ["nt%d" % k for k in range(8)]
     CW = ["cwA", "cwB", "cwZ"]
     nt, cw = R("nt", 0, VZ), R("cw", 0, VZ)
     dma("Y", [(T.nxi[:], T.nx[:])], [], ["nxi"], 1 << 18, pri=1e5)
@@ -167,18 +170,18 @@ def build(T, send):
     dma("S", [(T.wti[:], T.wt[:])], [], ["wti"], 512, pri=1e5)
     dma("S", [(T.zz[:, 0:L], T.z0[:])], [], [R("zz", 0, L)], 1 << 18, pri=1e5)
     dma("Y", [(T.cw[:, 0:V // 2], T.cards[:, 0:V // 2])], [], ["cwA"], 1 << 20, pri=5e4)
-    ms(R("nt", 0, 1536), 0.0, ["f0"])
-    ms(R("nt", 1536, 3840), 0.0, ["f1"])
-    act(R("nt", 3840, 5376), R("nt", 0, 1536), F.Copy, rd=["f0"], wr=["f2"])
-    act(R("nt", 5376, 6912), R("nt", 0, 1536), F.Copy, rd=["f0"], wr=["f4"])
+    ms(R("nt", 0, 1280), 0.0, ["f0"])
+    ms(R("nt", 1280, 4864), 0.0, ["f1"])
+    act(R("nt", 4864, 6144), R("nt", 0, 1280), F.Copy, rd=["f0"], wr=["f2"])
+    act(R("nt", 6144, 7168), R("nt", 0, 1024), F.Copy, rd=["f0"], wr=["f4"])
     iota(R("pi", 0, 1), [[0, 1]], 0, 1)
     iota(R("ti"), [[1, 144]], 0, 0)
-    iota(R("nt", 6912, VZ), [[0, VZ - 6912]], 0, 0, ["f3"])
+    iota(R("nt", 7168, VZ), [[0, VZ - 7168]], 0, 0, ["f3"])
     cp(R("nhi"), R("nxi"))
     tt(R("nlo"), R("nxi"), R("nhi"), A.subtract)
     zr = ["f1", "f2", "f3", "f4"]
     dma("Y", [(T.nt[0:128:16, 0:V], T.nhi[:])], ["nhi"] + zr, ["ntA", "f0"], 1 << 17)
-    dma("Y", [(T.nt[1:128:16, 0:V], T.nlo[:])], ["nlo"] + zr, ["ntB", "ntC", "ntD"], 1 << 17)
+    dma("Y", [(T.nt[1:128:16, 0:V], T.nlo[:])], ["nlo"] + zr, NT[1:], 1 << 17)
     dma("Y", [(T.cw[:, V // 2:V], T.cards[:, V // 2:V])], ["nlo"] + zr, ["cwB"], 1 << 20, pri=-1e5)
     cp(R("xo", 0, 64), R("curi"))
     ms(R("cw", V, VZ), 0.0, ["cwZ"])
@@ -188,7 +191,7 @@ def build(T, send):
     ts(R("pi", 4, 5), R("pi", 0, 1), 3, None, A.bitwise_and)
     ts(R("pi", 5, 6), R("pi", 0, 1), 15, 2, A.bitwise_and, A.logical_shift_right)
     cp(R("pf", 0, 6), R("pi", 0, 6))
-    ic, gi, par, p3, qc, g16, lo2, sw, cc, r2, wf, thr = (R("pf", k, k + 1) for k in range(1, 13))
+    ic, gi, par, p3, qc, g16, lo2, sw, cc, r2, wf, thr, th9, odd, lo4 = (R("pf", k, k + 1) for k in range(1, 16))
     ts(g16, gi, 16.0, None, A.mult)
     ts(lo2, ic, 1.5, None, A.is_lt)
     ts(R("zs"), R("ti"), 15.0, g16, A.subtract, A.is_equal)
@@ -200,24 +203,24 @@ def build(T, send):
     iota(R("jj"), [[16, 32]], 0, 1)
     iota(R("j8", 0, 32), [[16, 32]], V + VZ, 1)
     iota(R("j8", 32, 44), [[16, 12]], VZ, 1)
-    iota(R("jm"), [[16, 32]], -1535, 1)
-    iota(R("cp", 0, S), [[0, S]], 0, 0)
+    iota(R("jm"), [[16, 16]], Q - 2047, 1)
+    iota(R("cp", 0, S // 2), [[0, S // 2]], 0, 0)
     zero, idp, idn, big, bd = R("zer"), R("idp"), R("idn"), R("big"), R("bd")
     ms(zero, 0.0)
     rows = ((-16, 8), (0, 16))
     sel(big, zero, 0, A.not_equal, 16.0 * V)
     ts(bd, R("tg"), g16, None, A.is_equal)
-    ts(thr, ic, 9.0, 0.5, A.not_equal, A.subtract)
+    ts(th9, ic, 9.0, -100.0, A.is_equal, A.mult)
+    ts(thr, th9, 0.5, None, A.add)
     sel(idp, zero, 0, A.not_equal, 1.0)
     sel(idn, zero, 0, A.not_equal, -1.0)
     sel(blk("sc1", 0), zero, -8, A.not_equal, 0.25, rows)
     sel(blk("sc1", 1), blk("sc1", 0), -9, A.not_equal, -0.5, rows)
-    for i in range(8):
+    for i in range(4):
         sel(blk("selt", i), blk("sc1", 1), -i, A.not_equal, 0.25, rows)
     sel(R("sa"), zero, 16, A.not_equal, 1.0)
     sel(R("sh"), R("sa"), -112, A.not_equal, 1.0)
     ts(R("tih"), R("ti", 0, 66), -64.5, None, A.add)
-    iota(R("til"), [[1, 64]], -64, 0)
     ts(sw, par, -2.0, 1.0, A.mult, A.add)
     ts(R("swf"), R("di"), sw, None, A.is_equal)
     ts(cc, gi, 4.0, p3, A.mult, A.add)
@@ -227,32 +230,31 @@ def build(T, send):
     ts(r2, ic, 2.0, 16384.0, A.is_equal, A.mult)
     tt(R("zq", 0, 143), R("zs", 0, 143), R("zs", 1, 144), A.add)
     scaled(R("zp", 0, 143), R("zq", 0, 143), r2)
-    act(R("ua"), bd, F.Identity, scale=-1.0)
-    sel(R("ub"), R("ua"), 0, A.is_ge, 0.0)
-    sel(R("un"), R("ub"), 0, A.not_equal, -2048.0)
+    ts(odd, par, -1.0, None, A.add)
+    scaled(R("ua"), bd, odd)
+    act(R("uc"), R("ua"), F.Identity, scale=-1.0)
+    sel(R("ub"), R("ua"), 0, A.is_ge, 0.0, ((-16, 8), (0, 2), (-2, 8)))
+    sel(R("un"), R("ub"), 0, A.not_equal, -2048.0, ((-16, 8), (0, 2), (-2, 8)))
+    for e in range(2):
+        sel(blk("be", e), R("uc"), -e, A.is_equal, 0.0, ((0, 8), (1, 2), (0, 8)), 0)
+        sel(blk("ue", e), R("un"), -e, A.is_equal, 0.0, ((0, 8), (1, 2), (0, 8)), 0)
+        ts(blk("id2", e), R("di"), 2.0 * e, lo2, A.is_equal, A.mult)
+    ts(lo4, ic, 3.5, lo2, A.is_lt, A.subtract)
+    scaled(R("zd"), R("zs"), lo4)
     for d in range(7):
         sel(blk("shd", d), R("sh"), d + 1, A.is_equal if d else A.is_ge, 0.0, ((-1, 8), (0, 16)), 0)
     iota(R("one"), [[0, 32]], 1, 0)
     iota(R("sb", S + 12, W), [[0, W - S - 12]], 0, 0)
-    if OPT["fuse"]:
-        move(R("z4"), R("zz", 0, L), -0.25)
+    move(R("z4"), R("zz", 0, L), -0.25)
 
-    def xo(r, s, h=None):
-        return blk("xo", 9 * r + s, 64) if h is None else blk("xo", 18 * r + 2 * s + h, 32)
-
-    def cd(r, s, h):
-        return blk("cd", 18 * r + 2 * s - 2 + h, 512)
-
-    def zz(r, h):
-        return blk("zz", 2 * r + h, 512)
+    def xo(r, s):
+        return blk("xo", 9 * r + s, 64)
 
     def halves(o, win, off, rd, bias=0.0):
-        n = 1 if tag[0][:2] in OPT["whole"].split() else 2
         t = tag[0]
-        for h in range(n):
+        for h in range(2):
             tag[0] = t + str(h)
-            gather(R(o[0], o[1] + L // n * h, o[1] + L // n * (h + 1)), win, R(off[0], off[1] + 64 // n * h, off[1] + 64 // n * (h + 1)),
-                   rd, bias)
+            gather(R(o[0], o[1] + AC * h, o[1] + AC * (h + 1)), win, R(off[0], off[1] + 32 * h, off[1] + 32 * (h + 1)), rd, bias)
         tag[0] = t
 
     def listed(r, s):
@@ -261,86 +263,97 @@ def build(T, send):
             mm([(y, terms)])
             cp(xo(r, s), y)
             move(R("mn"), y, 7.0 * V)
+            return
+        if r and s <= raw:
+            tt(y, y, blk("mf", s - 1, 64), A.add)
         else:
             mm([(y, [(big, blk("mk", s - 1, 64), 1)] + terms)])
-            ts(xo(r, s), y, float(-V * (8 - s)), float(V), A.add, A.min)
-            tt(R("mn" if s < 8 else "um"), y, R("mn"), A.min)
+        ts(xo(r, s), y, float(-V * (8 - s)), float(V), A.add, A.min)
+        tt(R("mn" if s < 8 else "um"), y, R("mn"), A.min)
 
     def chase(r, steps):
-        raw = OPT["raw"] if r else 0
         for s in steps:
             tag[0] = "c%d%d" % (r, s)
-            halves(blk("gch", s - 1, L), nt, blk("xr", s - 1, 64) if 1 < s - 1 <= raw else xo(r, s - 1), NT)
-            if 1 < s <= raw:
+            if r:
+                gather(blk("gch", s - 1, L), nt, blk("xr", s - 1, 64) if 1 < s - 1 <= raw else xo(r, s - 1), NT)
+            else:
+                halves(blk("gch", s - 1, L), nt, xo(r, s - 1), NT)
+            if r and 1 < s <= raw:
                 mm([(blk("pch", s - 1, 64), wrap("zc", "gch", L * (s - 1), L * s))])
                 cp(blk("xr", s, 64), blk("pch", s - 1, 64))
-            elif s != raw + 1 or s == 1:
+            elif not r or s != raw + 1:
                 listed(r, s)
 
     def cards(r, steps):
         for s in steps:
             tag[0] = "k%d%d" % (r, s)
-            if OPT["fuse"] and (r, s) == (0, 1):
+            if (r, s) == (0, 1):
                 for h in range(2):
-                    gather_less(blk("dd", h, 512), cw, xo(r, s, h), CW, blk("z4", h, 512))
+                    gather_less(blk("dd", h, AC), cw, blk("xo", 2 + h, 32), CW, blk("z4", h, AC))
             else:
-                halves(blk("cd", 9 * r + s - 1, L), cw, xo(r, s), CW, 0.25 * min(s, 8))
+                halves(blk("cd", 9 * r + s - 1, L), cw, blk("xr", s, 64) if r and s in pens else xo(r, s), CW, 0.25 * min(s, 8))
 
     def turns(r):
         tag[0] = "t%d" % r
         mm([(R("pm1", 128, 192), wrap("zw", "zz", L * r, L * r + L))])
         cp(R("ci"), R("pm1", 128, 192))
         ts(R("cj"), R("ci"), 7, None, A.bitwise_and)
+        if r:
+            ts(R("mf", 0, 64), R("cj"), -16.0 * V, None, A.mult)
         for s in range(2, 9):
-            ts(blk("mk", s - 1, 64), R("cj"), s - 1.0, (8 - s) / 16, A.is_lt, A.max)
-        for s in range(2, OPT["raw"] + 2 if r else 0):
+            if r and s <= raw:
+                ts(blk("mf", s - 1, 64), R("mf", 0, 64), 16.0 * V * (s - 1), float(V * (8 - s)), A.add, A.max)
+            else:
+                ts(blk("mk", s - 1, 64), R("cj"), s - 1.0, (8 - s) / 16, A.is_lt, A.max)
+        for s in range(2, raw + 2 if r else 0):
             tag[0] = "l%d%d" % (r, s)
             listed(r, s)
 
     def cuts(r):
-        g2, tag[0] = L * r, "u%d" % r
+        g2, tag[0], early = L * r, "u%d" % r, OPT["early"][r] == "Y"
         ts(R("uu"), R("um"), V - 1, None, A.bitwise_and)
+        cp(R("uo"), R("uu"))
         for a in range(4):
             ts(blk("l4", a, 32), R("uu", 0, 32), float(V), R("q4", a, a + 1), A.add, A.mult)
-        cp(R("uo"), R("uu"))
         mm([(R("pm1", 64, 96), [(R("l4"), R("rs"), 1)])])
         move(R("hl", 0, 32), R("pm1", 64, 96), 32.5)
         tt(R("hl", 32, 64), R("pm1", 64, 96), R("hl", 0, 32), A.subtract)
-        mm([(R("pm1", 96, 128), [(R("swf"), blk("l4", a, 32), 1) for a in range(4)])], last=False)
+        ts(R("uf"), R("uu", 0, 32), float(V), None, A.add)
+        mm([(R("pm1", 96, 128), [(R("swf"), R("uf"), 1)])], last=False)
         tag[0] = "v%d" % r
         gather(blk("g2", 2 * r + 1, AC), nt, blk("uo", 1, 32), NT)
-        for k in range(2):
-            bank, h0, step = ("phb", "pm2")[k], 128 * k, OPT["step"][2 * r + k] == "S"
-            w = 65 if step else 64
-            for gq in range(4 * k, 4 * k + 4):
+
+        def reveal():
+            gather(blk("g2", 2 * r, AC), nt, blk("uo", 0, 32), NT)
+            mm([(R("pm2", 0, 64), wrap("zc", "g2", g2, g2 + L))])
+            cp(xo(r, 9), R("pm2", 0, 64))
+
+        if early:
+            reveal()
+        for k in range(4):
+            bank, h0, f0 = ("phb", "pm2")[k % 2], 128 * (k % 2) + 130 * (k // 2), 144 * k
+            for gq in (2 * k, 2 * k + 1):
                 tag[0] = "h%d%d" % (r, gq)
                 for c in range(4 * gq, 4 * gq + 4):
                     ts(blk("ohh", c), R("tib"), R("hl", c, c + 1), None, A.is_equal)
-                    lo, oh = R("hl", 32 + c, 33 + c), R("ohl", 66 * c, 66 * c + w)
-                    if step:
-                        ts(oh, R("tih", 0, w), lo, 2.0, A.is_lt, A.mult)
-                        act(oh, R("tih", 0, w), F.Sign, bias=lo, scale=-1.0)
-                        either()
-                    else:
-                        ts(oh, R("til"), lo, None, A.is_equal)
-                a = h0 + w * (gq % 4)
-                mm([(R(bank, a, a + w), [(blk("ohh", c), R("ohl", 66 * c, 66 * c + w), 1) for c in range(4 * gq, 4 * gq + 4)])])
-            f0, tag[0] = 260 * k, "m%d%d" % (r, k)
-            if step:
-                move(R("cs", f0, f0 + 260), R(bank, h0, h0 + 260), 3.0)
-                tt(R("fl", f0, f0 + 259), R(bank, h0, h0 + 259), R("cs", f0 + 1, f0 + 260), A.is_gt)
-            else:
-                ts(R("fl", f0, f0 + 256), R(bank, h0, h0 + 256), 1.5, None, A.is_gt)
-                act(R("fl", f0, f0 + 256), R(bank, h0, h0 + 256), F.Relu, bias=-1.0)
-                either()
-            dma("Y", [(T.nt[64 * k + 16 * j + 2:64 * k + 16 * j + 3, 0:V], T.fl[:, f0 + w * j:f0 + w * j + 64]) for j in range(4)],
-                [R("fl", f0, f0 + 260)], [NT[2 + k]], 1 << 16)
-        tag[0] = "v%d" % r
-        gather(blk("g2", 2 * r, AC), nt, blk("uo", 0, 32), NT)
-        mm([(R("pm2", 0, 64), wrap("zc", "g2", g2, g2 + L))])
-        cp(xo(r, 9), R("pm2", 0, 64))
-        tag[0] = "x%d" % r
-        mm([(R("pm1", 96, 128), [(R("zp", 14 - (i & 14), 142 - (i & 14)), R("g2", g2 + i, g2 + AC), 16) for i in range(16)])], False)
+                    lo, oh = R("hl", 32 + c, 33 + c), R("ohl", 66 * c, 66 * c + 65)
+                    ts(oh, R("tih", 0, 65), lo, 2.0, A.is_lt, A.mult)
+                    act(oh, R("tih", 0, 65), F.Sign, bias=lo, scale=-1.0)
+                    either()
+                a = h0 + 65 * (gq % 2)
+                mm([(R(bank, a, a + 65), [(blk("ohh", c), R("ohl", 66 * c, 66 * c + 65), 1) for c in range(4 * gq, 4 * gq + 4)])])
+            tag[0] = "m%d%d" % (r, k)
+            move(R("cs", f0, f0 + 130), R(bank, h0, h0 + 130), 3.0)
+            tt(R("fl", f0, f0 + 129), R(bank, h0, h0 + 129), R("cs", f0 + 1, f0 + 130), A.is_gt)
+            dma("Y", [(T.nt[32 * k + 16 * j + 2:32 * k + 16 * j + 3, 0:V], T.fl[:, f0 + 65 * j:f0 + 65 * j + 64]) for j in range(2)],
+                [R("fl", f0, f0 + 130)], NT[2 + 2 * k:4 + 2 * k], 1 << 15)
+        tag[0] = "x%d" % r if early else "v%d" % r
+        if early:
+            gather(R("g3"), nt, blk("uo", 0, 32), NT)
+        else:
+            reveal()
+        tag[0], (m, m0) = "x%d" % r, ("g3", 0) if early else ("g2", g2)
+        mm([(R("pm1", 96, 128), [(R("zp", 14 - (i & 14), 142 - (i & 14)), R(m, m0 + i, m0 + AC), 16) for i in range(16)])], False)
         if r == 0:
             ts(R("cut"), R("pm1", 96, 128), 2.0 * V, None, A.is_lt)
         tt(R("t1"), R("j8", 0, 32), R("pm1", 96, 128), A.min)
@@ -354,21 +367,25 @@ def build(T, send):
 
     def deal():
         tag[0] = "d0"
+        mm([(R("pch", 0, Q), [(blk("id2", e), R("g2", e, AC), 2) for e in range(2)])])
+        move(R("g4"), R("pch", 0, Q))
         add("V", lambda g: g.vector.tensor_tensor_scan(T.s1[:], T.one[:], T.cut[:], 0.0, A.mult, A.add),
             ["one", "cut"], ["s1"], vc(R("s1")))
-        mm([(R("pm2", 64, 96), [(bd, R("s1"), 1), (R("un"), R("cut"), 1)]), (R("pm2", 96, 97), [(bd, R("s1", 31, 32), 1)])])
-        tt(R("t2"), R("jm"), R("pm2", 64, 96), A.min)
+        mm([(R("pm2", 64, 80), [(blk(z, e), R(x, e, 32), 2) for e in range(2) for z, x in (("be", "s1"), ("ue", "cut"))]),
+            (R("pm2", 400, 401), [(bd, R("s1", 31, 32), 1)])])
+        tt(R("t2"), R("jm"), R("pm2", 64, 80), A.min)
         ts(R("o2"), R("t2"), 2047.0, None, A.add)
-        far, top, aim = R("sb", S, S + 12), R("pm2", 100, 112), R("pm2", 112, 124)
-        ts(R("cnt"), R("pm2", 96, 97), g16, None, A.add)
+        far, top, aim = R("sb", S, S + 12), R("pm2", 404, 416), R("pm2", 416, 428)
+        ts(R("cnt"), R("pm2", 400, 401), g16, None, A.add)
         ts(far, R("jj", 0, 12), R("cnt"), 4.0 * V, A.is_ge, A.mult)
-        scatter(R("cp"), R("o2"), R("g2", 0, AC), ["cp"])
-        mm([(top, wrap("zc", "cp", 0, S))])
+        scatter(R("cp"), R("o2"), R("g4"), ["cp"])
+        pairs = [(R(("zc", "zd")[i % 2], 15 - i, 143 - i), R("cp", i // 2, S // 2), 8) for i in range(16)]
+        mm([(top, pairs)])
         cp(R("to"), top)
         gather(R("sb", 0, S), cw, R("to"), CW)
         add("G", send, ["sb"], ["land"], (1000,), kind="r")
         tag[0] = "d1"
-        mm([(aim, wrap("zc", "cp", 0, S) + [(idp, far, 1)])], last=False)
+        mm([(aim, pairs + [(idp, far, 1)])], last=False)
         mm([(aim, [(blk("shd", d), R("land", W * d + S, W * d + S + 12), 1) for d in range(7)])], False)
         mm([(R("phb", 0, S), [(blk("shd", d), R("land", W * d, W * d + S), 1) for d in range(7)])])
         move(R("ar"), R("phb", 0, S))
@@ -380,49 +397,42 @@ def build(T, send):
         dma("G", [(T.nf[0:128:16, 0:V], T.nt[1:128:16, 0:V])], NT[1:2], ["nf"], 1 << 19, accum_op=A.add, max_dma_last_dim=4096)
 
     def walk(r):
-        fused = OPT["fuse"] and r == 0
-        parts, a, banks = [], 0, PSUM[:4]
-        for n in OPT["parts"][r]:
-            f, banks = banks[0], banks[1:]
-            if n > 4:
-                pd, banks = R(banks[0], 0, 64 * n), banks[1:]
-            else:
-                pd = R(f, 256, 256 + 64 * n)
-            parts.append((a, n, f, pd))
-            a += 64 * n
-
-        def cut(name, k, a, n):
-            return R(name, L * k + a, L * k + a + 64 * n)
-
-        for h, (a, n, pf, pd) in enumerate([] if fused else parts):
-            tag[0] = "w%d0%d" % (r, h)
-            mm([(pd, [(idp, cut("cd", 9 * r, a, n), 1), (idn, cut("zz", r, a, n), 1)])])
-            move(cut("dd", 0, a, n), pd)
+        for h in range(4 if r else 0):
+            pw, tag[0] = PSUM[h], "w%d0%d" % (r, h)
+            mm([(blk(pw, 1, Q), [(idp, blk("cd", 36 * r + h, Q), 1), (idn, blk("zz", 4 * r + h, Q), 1)])])
+            move(blk("dd", h, Q), blk(pw, 1, Q))
+            tag[0] = "p%d0%d" % (r, h)
+            mm([(R(pw, 0, 64), fold("zw", "zz", 4 * r + h))])
+            cp(blk("cq", h, 64), R(pw, 0, 64))
+            ts(blk("cq", 4 + h, 64), blk("cq", h, 64), 7, None, A.bitwise_and)
+            for s in pens:
+                ts(blk("pen", 4 * s + h, 64), blk("cq", 4 + h, 64), s - 1.0, 32.0, A.is_lt, A.mult)
         for s in range(1, 9):
-            for h, (a, n, pf, pd) in enumerate(parts):
-                tag[0] = "b%d%d%d" % (r, s, h)
-                d, b, rr, fs = cut("dd", 0, a, n), cut("bb", 0, a, n), cut("rr", 0, a, n), blk("fs", h, 64)
+            for h in range(4):
+                pw, tag[0] = PSUM[h], "b%d%d%d" % (r, s, h)
+                d, b, rr, fs, pd = blk("dd", h, Q), blk("bb", h, Q), blk("rr", h, Q), blk("fs", h, 64), blk(pw, 1, Q)
                 ts(b, d, 0.5, 0.5, A.is_gt, A.subtract)
                 act(b, d, F.Sign, bias=-0.5)
                 either()
-                mm([(R(pf, 0, 64), [(R("zs", 15 - i, 143 - i), cut("bb", 0, a + 64 * i, 1), 1) for i in range(n)])])
+                pen = [(idn, blk("pen", 4 * s + h, 64), 1)] if r and s in pens else []
+                mm([(R(pw, 0, 64), pen + fold("zs", "bb", h))])
                 tag[0] = "f%d%d%d" % (r, s, h)
-                ts(fs, R(pf, 0, 64), thr, 2.0, A.is_lt, A.mult)
-                act(fs, R(pf, 0, 64), F.Sign, bias=thr, scale=-1.0)
+                ts(fs, R(pw, 0, 64), thr, 2.0, A.is_lt, A.mult)
+                act(fs, R(pw, 0, 64), F.Sign, bias=thr, scale=-1.0)
                 either()
-                tag[0] = "w%d%d%d" % (r, s, h)
-                old = [(idn, d, 1), (idn, cut("zz", r, a, n), 1)] if fused and s == 1 else [(idn, cut("cd", 9 * r + s - 1, a, n), 1)]
-                mm([(pd, old + [(idp, cut("cd", 9 * r + s, a, n), 1)])])
-                mm([(blk(pf, i, 64), [(blk("selt", i), fs, 1)]) for i in range(n)])
-                tt(rr, d, R(pf, 0, 64 * n), A.mult)
+                tag[0], k = "w%d%d%d" % (r, s, h), 36 * r + 4 * s + h
+                old = [(idn, d, 1), (idn, blk("zz", h, Q), 1)] if (r, s) == (0, 1) else [(idn, blk("cd", k - 4, Q), 1)]
+                mm([(pd, old + [(idp, blk("cd", k, Q), 1)])])
+                mm([(blk(pw, i, 64), [(blk("selt", i), fs, 1)]) for i in range(4)])
+                tt(rr, d, blk(pw, 0, Q), A.mult)
                 if s < 8:
                     tt(d, rr, pd, A.add)
                 else:
-                    tt(cut("db", 0, a, n), rr, pd, A.add)
-                    act(cut("zz", r + 1, a, n), cut("db", 0, a, n), F.Abs)
-                    if r == 1 and (a + 64 * n) % 512 == 0:
-                        k = a // 512
-                        dma("Y", [(T.yz[:, 512 * k:512 * k + 512], ap(zz(2, k)))], [zz(2, k)], ["yz%d" % k], 1 << 17)
+                    z = blk("zz", 4 * r + 4 + h, Q)
+                    tt(blk("db", h, Q), rr, pd, A.add)
+                    act(z, blk("db", h, Q), F.Abs)
+                    if r:
+                        dma("Y", [(T.yz[:, Q * h:Q * h + Q], ap(z))], [z], ["yz%d" % h], 1 << 16)
 
     turns(0)
     chase(0, range(1, 9))
@@ -430,10 +440,10 @@ def build(T, send):
     cuts(0)
     cards(0, [9])
     deal()
-    chase(1, range(1, OPT["raw"] + 2))
+    chase(1, range(1, raw + 2))
     walk(0)
     turns(1)
-    chase(1, range(OPT["raw"] + 2, 9))
+    chase(1, range(raw + 2, 9))
     cards(1, range(1, 9))
     cuts(1)
     cards(1, [9])
@@ -446,7 +456,7 @@ def build(T, send):
 
 
 def depend(ops):
-    hist, deps = {}, []
+    hist, deps, above = {}, [], []
     for n, o in enumerate(ops):
         ds = set()
         for kind, rs in (("r", o["rd"]), ("w", o["wr"])):
@@ -460,8 +470,17 @@ def depend(ops):
                 if kind == "w":
                     h[:] = [e for e in h if not (a <= e[2] and e[3] <= b)]
                 h.append((n, kind, a, b))
-        deps.append(sorted(ds))
+        above.append(ds.union(*[above[m] for m in ds]))
+        deps.append([m for m in sorted(ds) if not any(m in above[j] for j in ds)])
     return deps
+
+
+def followers(deps):
+    succ = [[] for _ in deps]
+    for k, d in enumerate(deps):
+        for m in d:
+            succ[m].append(k)
+    return succ
 
 
 def lengths(ops, tm):
@@ -472,20 +491,15 @@ def lengths(ops, tm):
     return cost, lat
 
 
-def place(ops, deps, tm, urge, lean):
+def place(ops, deps, tm):
     n, wake = len(ops), tm["wake"]
     cost, lat = lengths(ops, tm)
     deps = [d + [o["after"]] if "after" in o else d for d, o in zip(deps, ops)]
-    succ, tail = [[] for _ in range(n)], [0.0] * n
-    for k in range(n):
-        for m in deps[k]:
-            succ[m].append(k)
+    succ, tail = followers(deps), [0.0] * n
     for k in range(n - 1, -1, -1):
         tail[k] = min(cost[k].values()) + lat[k] + wake + max([tail[j] for j in succ[k]] + [0.0])
     for k, o in enumerate(ops):
-        t = ("w" if o["tag"][0] in "bf" else o["tag"][0]) + o["tag"][1:2]
-        a, b = urge.get(t, (0, 0))
-        tail[k] += o["pri"] + 100 * (a + b * int(o["tag"][2:3] or 0) - urge.get("H" + t, (0,))[0] * int(o["tag"][3:4] or 0))
+        tail[k] += o["pri"] + 100 * (URGE.get(o["tag"][:2], 0) - (STAGGER * int(o["tag"][3]) if o["tag"][0] in "bfw" else 0))
     left, busy, start, end, eng = [len(d) for d in deps], {}, [0.0] * n, [0.0] * n, [None] * n
     ready = [k for k in range(n) if not left[k]]
     while ready:
@@ -502,7 +516,7 @@ def place(ops, deps, tm, urge, lean):
                         pad = 0.0 if key == q else wake
                         if a - pad < t + c and b + pad > t and (key == q or q2 != q):
                             t, again = b + pad, True
-            v = t + c - (100 * lean.get(ops[k]["tag"][:2], 0) if q == "V" else 0)
+            v = t + c - (100 * LEAN.get(ops[k]["tag"][:2], 0) if q == "V" else 0)
             if best is None or v < best[0]:
                 best = v, t, q
         start[k], eng[k] = best[1:]
@@ -516,28 +530,26 @@ def place(ops, deps, tm, urge, lean):
     return sorted(range(n), key=lambda x: (start[x], x)), eng
 
 
-def refine(ops, deps, tm, order, eng, tries, heat, seed=1):
-    n, wake, near = len(ops), tm["wake"], tm["wake"] - tm["same"]
-    cost, lat = lengths(ops, tm)
-    above = []
-    for k in range(n):
-        above.append(set(deps[k]).union(*[above[m] for m in deps[k]]))
-    need = [[m for m in deps[k] if not any(m in above[j] for j in deps[k])] for k in range(n)]
-    succ, prec = [[] for _ in range(n)], [d + [o["after"]] if "after" in o else d for d, o in zip(need, ops)]
-    for k in range(n):
-        for m in prec[k]:
-            succ[m].append(k)
-    banks, flex, rnd = [o["banks"] for o in ops], [k for k in range(n) if len(cost[k]) > 1], [seed]
+def refine(ops, need, tms, order, eng, tries, heat, seed=1):
+    n = len(ops)
+    prec = [d + [o["after"]] if "after" in o else d for d, o in zip(need, ops)]
+    succ, after = followers(prec), followers(need)
+    banks, flex, rnd = [o["banks"] for o in ops], [k for k in range(n) if len(ops[k]["on"]) > 1], [seed]
+    sizes = [lengths(ops, tm) + (tm["wake"], tm["wake"] - tm["same"]) for tm in tms]
 
     def pick(m):
         rnd[0] = (rnd[0] * 1103515245 + 12345) % 2147483648
         return (rnd[0] >> 8) % m
 
-    def run(order, eng, first, marks, end, why):
+    def run(size, order, eng, first, last, limit, marks, end, why, rest):
+        cost, lat, wake, near = size
         i0 = first // 32
-        held, marks, end, why = dict(marks[i0]), marks[:i0], end[:], why[:]
+        held, old, marks, end, why, reach = dict(marks[i0]), marks, marks[:i0], end[:], why[:], last
         for i in range(32 * i0, n):
             if i % 32 == 0:
+                if i > reach and held == old[i // 32]:
+                    marks += old[i // 32:]
+                    break
                 marks.append(dict(held))
             k = order[i]
             q = eng[k]
@@ -550,30 +562,65 @@ def refine(ops, deps, tm, order, eng, tries, heat, seed=1):
                 e = held[b]
                 if e[1] != q and e[0] + wake > t:
                     t, w = e[0] + wake, e[2]
+            if i > last and t + rest[k] > limit:
+                return None
             t += cost[k][q]
             e = held[q] = (t, q, k)
             for b in banks[k]:
                 held[b] = e
-            end[k], why[k] = t + lat[k] + wake, w
-        return max(end), marks, end, why
+            t += lat[k] + wake
+            if t != end[k]:
+                end[k] = t
+                for j in after[k]:
+                    if pos[j] > reach:
+                        reach = pos[j]
+            why[k] = w
+        top = max(end)
+        return [top + 0.3 * sum(end) / n, top, marks, end, why]
 
-    now = run(order, eng, 0, [{x: (0.0, x, None) for x in list("VSPGY") + PSUM}], [0.0] * n, [None] * n)
-    best, fresh = (now[0], order, eng), True
+    def back(size, order, eng):
+        cost, lat, wake, near = size
+        rest, nxt = [0.0] * n, {}
+        for k in order[::-1]:
+            q = eng[k]
+            t = lat[k] + wake
+            e = max(nxt.get(q, 0.0), t)
+            for j in after[k]:
+                x = t + rest[j] - near if eng[j] == q else t + rest[j]
+                if x > e:
+                    e = x
+            for b in banks[k]:
+                x = nxt.get(b)
+                if x and x[1] != q and x[0] + wake > e:
+                    e = x[0] + wake
+            e = nxt[q] = rest[k] = cost[k][q] + e
+            for b in banks[k]:
+                nxt[b] = (e, q)
+        return rest
+
+    pos, taken = {x: i for i, x in enumerate(order)}, 0
+    now = [run(s, order, eng, 0, n, 0, [{x: (0.0, x, None) for x in list("VSPGY") + PSUM}], [0.0] * n, [None] * n, None)
+           + [back(s, order, eng)] for s in sizes]
+    total = sum(x[0] for x in now)
+    best, fresh, held_up = (total, order, eng), True, [(1, 0)]
     for it in range(tries):
         if fresh:
-            k, chain, fresh, pos = now[2].index(now[0]), [], False, {x: i for i, x in enumerate(order)}
-            while now[3][k] is not None:
-                chain.append((now[3][k], k))
-                k = now[3][k]
-            held_up = [p for p in chain if p[0] not in need[p[1]]]
-            loose = [p[1] for p in chain if len(cost[p[1]]) > 1] or flex
-        o2, e2, kind, far = order, eng, pick(20), (0, 0, 0, 2, 5, 12, 30)[pick(7)]
+            one = now[pick(len(now))]
+            k, chain = one[3].index(one[1]) if pick(10) >= 3 else pick(n), []
+            while one[4][k] is not None:
+                chain.append((one[4][k], k))
+                k = one[4][k]
+            held_up = [p for p in chain if p[0] not in need[p[1]]] or held_up
+            loose = [p[1] for p in chain if len(ops[p[1]]["on"]) > 1] or flex
+        o2, e2, kind, far, fresh = order, eng, pick(20), (0, 0, 0, 2, 5, 12, 30)[pick(7)], pick(30) == 0
         if kind < 3:
             k = flex[pick(len(flex))] if kind == 0 else loose[pick(len(loose))]
-            e2, a = eng[:], pos[k]
+            e2, a, b = eng[:], pos[k], max([pos[k]] + [pos[j] for j in after[k]])
             e2[k] = "V" if eng[k] == "S" else "S"
         else:
             x, y = held_up[pick(len(held_up))]
+            if pos[x] > pos[y]:
+                continue
             up = kind < 12
             a, b = (max(0, pos[x] - far), pos[y]) if up else (pos[x], min(n - 1, pos[y] + far))
             seg, mv = order[a:b + 1], {y if up else x}
@@ -583,18 +630,28 @@ def refine(ops, deps, tm, order, eng, tries, heat, seed=1):
             if (x if up else y) in mv:
                 continue
             o2 = order[:a] + [j for j in seg if (j in mv) == up] + [j for j in seg if (j in mv) != up] + order[b + 1:]
-        new = run(o2, e2, a, *now[1:])
-        if new[0] <= now[0] + heat * (1 - it / tries) * pick(1000) / 1000:
-            order, eng, now, fresh = o2, e2, new, True
-            if new[0] < best[0]:
-                best = new[0], o2, e2
+        room, new = heat * (1 - it / tries) * pick(1000) / 1000, []
+        for s, old in zip(sizes, now):
+            new.append(run(s, o2, e2, a, b, old[1] + 3 * room + 100, *old[2:]))
+            if new[-1] is None:
+                break
+        if new[-1] and sum(x[0] for x in new) <= total + room * len(now):
+            order, eng, fresh, total, taken = o2, e2, True, sum(x[0] for x in new), taken + 1
+            now = [x + [back(s, order, eng) if taken % 8 == 0 else y[5]] for s, x, y in zip(sizes, new, now)]
+            for i in range(a, b + 1):
+                pos[order[i]] = i
+            if total < best[0]:
+                best = total, o2, e2
     return best[1:]
 
 
 def plan(ops):
     if not PLAN:
         deps = depend(ops)
-        PLAN["p"] = refine(ops, deps, TIME, *place(ops, deps, TIME, URGE, LEAN), *TRIES) + (deps,)
+        got = place(ops, deps, dict(TIMES[0], cy=0.84, pc=0.40, ga=1.45, sc=3.2))
+        for t in TRIES:
+            got = refine(ops, deps, TIMES, *got, *t)
+        PLAN["p"] = got + (deps,)
     return PLAN["p"]
 
 

from concourse.bass import DstId, RemoteDMATransfer
from concourse.mybir import AluOpType as A, ActivationFunctionType as F

V, L, AC, S, W, Q = 8192, 1024, 512, 192, 208, 256
VZ = V + 16
BF, F32, I32, U16, F16 = "bfloat16", "float32", "int32", "uint16", "float16"
SCRATCH = {}
for _dt, _bufs in (
        (BF, dict(cw=VZ + S + 128, nt=VZ + AC + 128, nhi=512, nlo=512, zz=3 * L, gch=8 * L, g2=2 * L, g3=AC, db=L, bb=L, fs=256,
                  pen=1024, mk=512, hl=64, ohh=32 * 128, ohl=32 * 66, fl=576, cut=32, s1=32, g4=Q, cp=AC + 128, sb=W, land=7 * W, ar=S,
                  tib=128, tih=66, zs=144, zc=144, zw=144, zq=144, zp=144, idp=128, idn=128, big=128, bd=128, selt=512,
                  zer=128, sc1=256, zd=144, id2=256, be=256, ue=256, ua=128, ub=128, uc=128, un=128, sa=128, sh=128, shd=7 * 128, one=32)),
        (F16, dict(cd=18 * L, dd=L, z4=L)),
        (I32, dict(nxi=512, curi=64, wti=1, rr=L, ci=64, cj=64, cq=512, um=64, uu=64, pi=8)),
        (U16, dict(xo=19 * 64, xr=8 * 64, uo=64, o1=32, o2=16, o3=12, to=12)),
        (F32, dict(nf=VZ + AC + 128, vf=AC, mf=512, uf=32, mn=64, l4=128, cs=576, t1=32, t2=16, cnt=1, t5=12, pf=16, ti=144,
                   di=128, tg=128, jj=32, j8=44, jm=16, swf=128, q4=4, rs=32))):
    for _k in _bufs:
        SCRATCH[_k] = ("sbuf", [128, _bufs[_k]], _dt)
PSUM = ["pw0", "pw1", "pw2", "pw3", "pch", "pm1", "pm2", "phb"]
for _k in PSUM:
    SCRATCH[_k] = ("psum", [128, 512], F32)
SEMAPHORES = ["qV", "qS", "qP", "qG", "arr", "sent"] + ["d%d" % i for i in range(32)]

OPT = dict(raw=5, pen=2, early="NY")
TIMES = [dict(cy=1.00, pc=0.46, ga=1.9, sc=4.2, wake=235.0, same=100.0, dma=1150.0, rate=480.0, send=4300.0, call=dict(V=3.0, S=15.0, P=35.0)),
         dict(cy=0.95, pc=0.46, ga=1.2, sc=2.5, wake=176.0, same=160.0, dma=1330.0, rate=570.0, send=5900.0, call=dict(V=0.0, S=15.0, P=41.0)),
         dict(cy=0.83, pc=0.30, ga=1.5, sc=2.4, wake=286.0, same=55.0, dma=1300.0, rate=530.0, send=3400.0, call=dict(V=0.0, S=15.0, P=27.0))]
URGE = dict(t0=1000, c0=1000, u0=1000, h0=1000, m0=1000, v0=1000, x0=1010, d0=1000, d1=1000, k0=20,
            c1=300, t1=500, l1=300, u1=300, v1=300, k1=10)
STAGGER = 5
LEAN = dict(a=-20, c0=5, k0=-90, c1=-90, k1=-90, v0=-90, v1=-90, b0=10, f0=5, f1=5, h0=-2, h1=-10, m1=-5, w1=-5, x1=-10)
TRIES = ((125000, 100.0, 3), (120000, 100.0, 4))
PLAN = {}


def build(T, send):
    ops, tag, loads = [], ["a"], []
    raw, pens = OPT["raw"], range(2, OPT["pen"] + 1)

    def R(name, a=0, b=None):
        return (name, a, (SCRATCH[name][1][1] if name in SCRATCH else 1) if b is None else b)

    def add(q, fn, rd, wr, size, kind="c", nbytes=0, pri=0.0):
        rd, wr = ([R(x) if isinstance(x, str) else x for x in l] for l in (rd, wr))
        ops.append(dict(on={q: (fn, (tuple(size) + (0, 0, 0, 0))[:5])}, rd=rd, wr=wr, kind=kind, nbytes=nbytes, pri=pri, tag=tag[0],
                        banks=sorted(set(r[0] for r in rd + wr if r[0] in PSUM))))

    def either():
        o = ops.pop()
        ops[-1]["on"].update(o["on"])
        ops[-1]["rd"] += [r for r in o["rd"] if r not in ops[-1]["rd"]]

    def ap(r):
        return T[r[0]][:, r[1]:r[2]]

    def vc(i, f=1.0):
        return 0, max(8, (i[2] - i[1]) * f)

    def two(*rs):
        return 0.5 if all(SCRATCH[r[0]][2] in (BF, F16, U16) for r in rs) else 1.0

    def cols(x):
        return [x] if isinstance(x, tuple) else []

    def sval(x):
        return ap(x) if isinstance(x, tuple) else x

    def ts(o, i, s1, s2, op0, op1=None):
        def fn(g):
            if op1 is None:
                return g.vector.tensor_scalar(ap(o), ap(i), sval(s1), None, op0)
            return g.vector.tensor_scalar(ap(o), ap(i), sval(s1), sval(s2), op0, op1)
        add("V", fn, [i] + cols(s1) + cols(s2), [o], vc(i, two(o, i)))

    def tt(o, a, b, op):
        add("V", lambda g: g.vector.tensor_tensor(ap(o), ap(a), ap(b), op), [a, b], [o],
            vc(a, 1.0 if (a[0] in PSUM or b[0] in PSUM) else 2.0))

    def cp(o, i):
        add("V", lambda g: g.vector.tensor_copy(ap(o), ap(i)), [i], [o], vc(i, two(o, i)))

    def ms(o, val, wr=None):
        add("V", lambda g: g.vector.memset(ap(o), val), [], wr or [o], vc(o, two(o)))

    def act(o, i, func, bias=0.0, scale=1.0, rd=None, wr=None):
        add("S", lambda g: g.scalar.activation(ap(o), ap(i), func, bias=sval(bias), scale=sval(scale)),
            (rd or [i]) + cols(bias) + cols(scale), wr or [o], vc(i))

    def move(o, i, bias=0.0):
        if bias:
            ts(o, i, bias, None, A.add)
        else:
            cp(o, i)
        act(o, i, F.Identity, bias=bias)
        either()

    def scaled(o, i, col):
        ts(o, i, col, None, A.mult)
        act(o, i, F.Identity, scale=col)
        either()

    def gather(o, win, off, rd, bias=0.0):
        def on_v(g):
            src = ap(win).indirect(ap(off))
            return g.vector.tensor_scalar(ap(o), src, bias, None, A.add) if bias else g.vector.tensor_copy(ap(o), src)
        add("V", on_v, rd + [off], [o], (50, 0, o[2] - o[1]))
        add("S", lambda g: g.scalar.activation(ap(o), ap(win).indirect(ap(off)), F.Identity, bias=bias), rd + [off], [o],
            (65, 0, o[2] - o[1]))
        either()

    def gather_less(o, win, off, rd, b):
        add("V", lambda g: g.vector.tensor_tensor(ap(o), ap(win).indirect(ap(off)), ap(b), A.subtract), rd + [off, b], [o],
            (50, 0, o[2] - o[1]))

    def scatter(win, off, i, wr):
        add("V", lambda g: g.vector.tensor_copy(ap(win).indirect(ap(off)), ap(i)), [off, i], wr, (50, 0, 0, i[2] - i[1]))

    def iota(o, pat, base, cm, wr=None):
        kw = {} if SCRATCH[o[0]][2] == I32 else dict(allow_small_or_imprecise_dtypes=True)
        add("G", lambda g: g.iota(ap(o), pat, base, cm, **kw), [], wr or [o], (130, 2 * (o[2] - o[1])))

    def sel(o, i, base, op, fill, pat=((-1, 128),), cm=1):
        add("G", lambda g: g.affine_select(ap(o), ap(i), [list(x) for x in pat], op, fill, base, cm), [i], [o], (170, 256))

    def mm(groups, first=True, last=True):
        rd, wr, cyc = [], [], 0
        (rd if first and last else wr).append("open" + groups[0][0][0])
        for o, terms in groups:
            wr.append(o)
            for l, r, st in terms:
                rd += [l, r]
                cyc += max(64, o[2] - o[1]) * (4 if SCRATCH[l[0]][2] == F32 else 1)

        def fn(g):
            ins = None
            for o, terms in groups:
                for k, (l, r, st) in enumerate(terms):
                    rhs = ap(r) if st == 1 else T[r[0]][:, r[1]:r[2]:st]
                    ins = g.tensor.matmul(ap(o), ap(l), rhs, first and k == 0, last and k == len(terms) - 1)
            return ins
        add("P", fn, rd, wr, (0, 0, 0, 0, cyc))

    def dma(q, pairs, rd, wr, nbytes, pri=0.0, **kw):
        def fn(g, sem):
            e = g if q == "G" else (g.sync if q == "Y" else g.scalar)
            for o, i in pairs:
                e.dma_start(o, i, **kw).then_inc(sem, 16)
            return 16 * len(pairs)
        add(q, fn, rd, wr, ((600 if q == "G" else 100) * len(pairs),), kind="d", nbytes=nbytes, pri=pri)
        if tag[0] == "a":
            if loads:
                ops[-1]["after"] = loads[-1]
            loads.append(len(ops) - 1)

    def blk(name, k, n=128):
        return R(name, n * k, n * k + n)

    def wrap(z, src, a, b):
        return [(R(z, 15 - i, 143 - i), R(src, a + i, b), 16) for i in range(16)]

    def fold(z, src, k):
        return [(R(z, 15 - i, 143 - i), blk(src, 4 * k + i, 64), 1) for i in range(4)]

    NT = ["ntA", "ntB"] + ["nt%d" % k for k in range(8)]
    CW = ["cwA", "cwB", "cwZ"]
    nt, cw = R("nt", 0, VZ), R("cw", 0, VZ)
    dma("Y", [(T.nxi[:], T.nx[:])], [], ["nxi"], 1 << 18, pri=1e5)
    dma("S", [(T.curi[:], T.cur[:])], [], ["curi"], 1 << 15, pri=1e5)
    dma("S", [(T.wti[:], T.wt[:])], [], ["wti"], 512, pri=1e5)
    dma("S", [(T.zz[:, 0:L], T.z0[:])], [], [R("zz", 0, L)], 1 << 18, pri=1e5)
    dma("Y", [(T.cw[:, 0:V // 2], T.cards[:, 0:V // 2])], [], ["cwA"], 1 << 20, pri=5e4)
    ms(R("nt", 0, 1280), 0.0, ["f0"])
    ms(R("nt", 1280, 4864), 0.0, ["f1"])
    act(R("nt", 4864, 6144), R("nt", 0, 1280), F.Copy, rd=["f0"], wr=["f2"])
    act(R("nt", 6144, 7168), R("nt", 0, 1024), F.Copy, rd=["f0"], wr=["f4"])
    iota(R("pi", 0, 1), [[0, 1]], 0, 1)
    iota(R("ti"), [[1, 144]], 0, 0)
    iota(R("nt", 7168, VZ), [[0, VZ - 7168]], 0, 0, ["f3"])
    cp(R("nhi"), R("nxi"))
    tt(R("nlo"), R("nxi"), R("nhi"), A.subtract)
    zr = ["f1", "f2", "f3", "f4"]
    dma("Y", [(T.nt[0:128:16, 0:V], T.nhi[:])], ["nhi"] + zr, ["ntA", "f0"], 1 << 17)
    dma("Y", [(T.nt[1:128:16, 0:V], T.nlo[:])], ["nlo"] + zr, NT[1:], 1 << 17)
    dma("Y", [(T.cw[:, V // 2:V], T.cards[:, V // 2:V])], ["nlo"] + zr, ["cwB"], 1 << 20, pri=-1e5)
    cp(R("xo", 0, 64), R("curi"))
    ms(R("cw", V, VZ), 0.0, ["cwZ"])
    ts(R("pi", 1, 2), R("pi", 0, 1), 15, None, A.bitwise_and)
    ts(R("pi", 2, 3), R("pi", 0, 1), 4, None, A.logical_shift_right)
    ts(R("pi", 3, 4), R("pi", 0, 1), 1, None, A.bitwise_and)
    ts(R("pi", 4, 5), R("pi", 0, 1), 3, None, A.bitwise_and)
    ts(R("pi", 5, 6), R("pi", 0, 1), 15, 2, A.bitwise_and, A.logical_shift_right)
    cp(R("pf", 0, 6), R("pi", 0, 6))
    ic, gi, par, p3, qc, g16, lo2, sw, cc, r2, wf, thr, th9, odd, lo4 = (R("pf", k, k + 1) for k in range(1, 16))
    ts(g16, gi, 16.0, None, A.mult)
    ts(lo2, ic, 1.5, None, A.is_lt)
    ts(R("zs"), R("ti"), 15.0, g16, A.subtract, A.is_equal)
    scaled(R("zc"), R("zs"), lo2)
    cp(wf, R("wti"))
    scaled(R("zw"), R("zs"), wf)
    iota(R("di"), [[1, 128]], 0, -1)
    iota(R("tg"), [[16, 8], [0, 16]], 0, 0)
    iota(R("jj"), [[16, 32]], 0, 1)
    iota(R("j8", 0, 32), [[16, 32]], V + VZ, 1)
    iota(R("j8", 32, 44), [[16, 12]], VZ, 1)
    iota(R("jm"), [[16, 16]], Q - 2047, 1)
    iota(R("cp", 0, S // 2), [[0, S // 2]], 0, 0)
    zero, idp, idn, big, bd = R("zer"), R("idp"), R("idn"), R("big"), R("bd")
    ms(zero, 0.0)
    rows = ((-16, 8), (0, 16))
    sel(big, zero, 0, A.not_equal, 16.0 * V)
    ts(bd, R("tg"), g16, None, A.is_equal)
    ts(th9, ic, 9.0, -100.0, A.is_equal, A.mult)
    ts(thr, th9, 0.5, None, A.add)
    sel(idp, zero, 0, A.not_equal, 1.0)
    sel(idn, zero, 0, A.not_equal, -1.0)
    sel(blk("sc1", 0), zero, -8, A.not_equal, 0.25, rows)
    sel(blk("sc1", 1), blk("sc1", 0), -9, A.not_equal, -0.5, rows)
    for i in range(4):
        sel(blk("selt", i), blk("sc1", 1), -i, A.not_equal, 0.25, rows)
    sel(R("sa"), zero, 16, A.not_equal, 1.0)
    sel(R("sh"), R("sa"), -112, A.not_equal, 1.0)
    ts(R("tih"), R("ti", 0, 66), -64.5, None, A.add)
    ts(sw, par, -2.0, 1.0, A.mult, A.add)
    ts(R("swf"), R("di"), sw, None, A.is_equal)
    ts(cc, gi, 4.0, p3, A.mult, A.add)
    ts(R("rs"), R("ti", 0, 32), cc, None, A.is_equal)
    ts(R("q4"), R("ti", 0, 4), qc, None, A.is_equal)
    iota(R("tib"), [[64, 128]], V + 64, 0)
    ts(r2, ic, 2.0, 16384.0, A.is_equal, A.mult)
    tt(R("zq", 0, 143), R("zs", 0, 143), R("zs", 1, 144), A.add)
    scaled(R("zp", 0, 143), R("zq", 0, 143), r2)
    ts(odd, par, -1.0, None, A.add)
    scaled(R("ua"), bd, odd)
    act(R("uc"), R("ua"), F.Identity, scale=-1.0)
    sel(R("ub"), R("ua"), 0, A.is_ge, 0.0, ((-16, 8), (0, 2), (-2, 8)))
    sel(R("un"), R("ub"), 0, A.not_equal, -2048.0, ((-16, 8), (0, 2), (-2, 8)))
    for e in range(2):
        sel(blk("be", e), R("uc"), -e, A.is_equal, 0.0, ((0, 8), (1, 2), (0, 8)), 0)
        sel(blk("ue", e), R("un"), -e, A.is_equal, 0.0, ((0, 8), (1, 2), (0, 8)), 0)
        ts(blk("id2", e), R("di"), 2.0 * e, lo2, A.is_equal, A.mult)
    ts(lo4, ic, 3.5, lo2, A.is_lt, A.subtract)
    scaled(R("zd"), R("zs"), lo4)
    for d in range(7):
        sel(blk("shd", d), R("sh"), d + 1, A.is_equal if d else A.is_ge, 0.0, ((-1, 8), (0, 16)), 0)
    iota(R("one"), [[0, 32]], 1, 0)
    iota(R("sb", S + 12, W), [[0, W - S - 12]], 0, 0)
    move(R("z4"), R("zz", 0, L), -0.25)

    def xo(r, s):
        return blk("xo", 9 * r + s, 64)

    def halves(o, win, off, rd, bias=0.0):
        t = tag[0]
        for h in range(2):
            tag[0] = t + str(h)
            gather(R(o[0], o[1] + AC * h, o[1] + AC * (h + 1)), win, R(off[0], off[1] + 32 * h, off[1] + 32 * (h + 1)), rd, bias)
        tag[0] = t

    def listed(r, s):
        y, terms = blk("pch", s - 1, 64), wrap("zc", "gch", L * (s - 1), L * s)
        if s == 1:
            mm([(y, terms)])
            cp(xo(r, s), y)
            move(R("mn"), y, 7.0 * V)
            return
        if r and s <= raw:
            tt(y, y, blk("mf", s - 1, 64), A.add)
        else:
            mm([(y, [(big, blk("mk", s - 1, 64), 1)] + terms)])
        ts(xo(r, s), y, float(-V * (8 - s)), float(V), A.add, A.min)
        tt(R("mn" if s < 8 else "um"), y, R("mn"), A.min)

    def chase(r, steps):
        for s in steps:
            tag[0] = "c%d%d" % (r, s)
            if r:
                gather(blk("gch", s - 1, L), nt, blk("xr", s - 1, 64) if 1 < s - 1 <= raw else xo(r, s - 1), NT)
            else:
                halves(blk("gch", s - 1, L), nt, xo(r, s - 1), NT)
            if r and 1 < s <= raw:
                mm([(blk("pch", s - 1, 64), wrap("zc", "gch", L * (s - 1), L * s))])
                cp(blk("xr", s, 64), blk("pch", s - 1, 64))
            elif not r or s != raw + 1:
                listed(r, s)

    def cards(r, steps):
        for s in steps:
            tag[0] = "k%d%d" % (r, s)
            if (r, s) == (0, 1):
                for h in range(2):
                    gather_less(blk("dd", h, AC), cw, blk("xo", 2 + h, 32), CW, blk("z4", h, AC))
            else:
                halves(blk("cd", 9 * r + s - 1, L), cw, blk("xr", s, 64) if r and s in pens else xo(r, s), CW, 0.25 * min(s, 8))

    def turns(r):
        tag[0] = "t%d" % r
        mm([(R("pm1", 128, 192), wrap("zw", "zz", L * r, L * r + L))])
        cp(R("ci"), R("pm1", 128, 192))
        ts(R("cj"), R("ci"), 7, None, A.bitwise_and)
        if r:
            ts(R("mf", 0, 64), R("cj"), -16.0 * V, None, A.mult)
        for s in range(2, 9):
            if r and s <= raw:
                ts(blk("mf", s - 1, 64), R("mf", 0, 64), 16.0 * V * (s - 1), float(V * (8 - s)), A.add, A.max)
            else:
                ts(blk("mk", s - 1, 64), R("cj"), s - 1.0, (8 - s) / 16, A.is_lt, A.max)
        for s in range(2, raw + 2 if r else 0):
            tag[0] = "l%d%d" % (r, s)
            listed(r, s)

    def cuts(r):
        g2, tag[0], early = L * r, "u%d" % r, OPT["early"][r] == "Y"
        ts(R("uu"), R("um"), V - 1, None, A.bitwise_and)
        cp(R("uo"), R("uu"))
        for a in range(4):
            ts(blk("l4", a, 32), R("uu", 0, 32), float(V), R("q4", a, a + 1), A.add, A.mult)
        mm([(R("pm1", 64, 96), [(R("l4"), R("rs"), 1)])])
        move(R("hl", 0, 32), R("pm1", 64, 96), 32.5)
        tt(R("hl", 32, 64), R("pm1", 64, 96), R("hl", 0, 32), A.subtract)
        ts(R("uf"), R("uu", 0, 32), float(V), None, A.add)
        mm([(R("pm1", 96, 128), [(R("swf"), R("uf"), 1)])], last=False)
        tag[0] = "v%d" % r
        gather(blk("g2", 2 * r + 1, AC), nt, blk("uo", 1, 32), NT)

        def reveal():
            gather(blk("g2", 2 * r, AC), nt, blk("uo", 0, 32), NT)
            mm([(R("pm2", 0, 64), wrap("zc", "g2", g2, g2 + L))])
            cp(xo(r, 9), R("pm2", 0, 64))

        if early:
            reveal()
        for k in range(4):
            bank, h0, f0 = ("phb", "pm2")[k % 2], 128 * (k % 2) + 130 * (k // 2), 144 * k
            for gq in (2 * k, 2 * k + 1):
                tag[0] = "h%d%d" % (r, gq)
                for c in range(4 * gq, 4 * gq + 4):
                    ts(blk("ohh", c), R("tib"), R("hl", c, c + 1), None, A.is_equal)
                    lo, oh = R("hl", 32 + c, 33 + c), R("ohl", 66 * c, 66 * c + 65)
                    ts(oh, R("tih", 0, 65), lo, 2.0, A.is_lt, A.mult)
                    act(oh, R("tih", 0, 65), F.Sign, bias=lo, scale=-1.0)
                    either()
                a = h0 + 65 * (gq % 2)
                mm([(R(bank, a, a + 65), [(blk("ohh", c), R("ohl", 66 * c, 66 * c + 65), 1) for c in range(4 * gq, 4 * gq + 4)])])
            tag[0] = "m%d%d" % (r, k)
            move(R("cs", f0, f0 + 130), R(bank, h0, h0 + 130), 3.0)
            tt(R("fl", f0, f0 + 129), R(bank, h0, h0 + 129), R("cs", f0 + 1, f0 + 130), A.is_gt)
            dma("Y", [(T.nt[32 * k + 16 * j + 2:32 * k + 16 * j + 3, 0:V], T.fl[:, f0 + 65 * j:f0 + 65 * j + 64]) for j in range(2)],
                [R("fl", f0, f0 + 130)], NT[2 + 2 * k:4 + 2 * k], 1 << 15)
        tag[0] = "x%d" % r if early else "v%d" % r
        if early:
            gather(R("g3"), nt, blk("uo", 0, 32), NT)
        else:
            reveal()
        tag[0], (m, m0) = "x%d" % r, ("g3", 0) if early else ("g2", g2)
        mm([(R("pm1", 96, 128), [(R("zp", 14 - (i & 14), 142 - (i & 14)), R(m, m0 + i, m0 + AC), 16) for i in range(16)])], False)
        if r == 0:
            ts(R("cut"), R("pm1", 96, 128), 2.0 * V, None, A.is_lt)
        tt(R("t1"), R("j8", 0, 32), R("pm1", 96, 128), A.min)
        ts(R("o1"), R("t1"), -float(V), None, A.add)
        if r == 0:
            scatter(R("nt"), R("o1"), R("g2", 0, AC), NT)
        else:
            mm([(R("phb"), [(R("zc", 15, 143), R("g2", L, L + AC), 1)])])
            move(R("vf"), R("phb"))
            scatter(R("nf"), R("o1"), R("vf"), ["nf"])

    def deal():
        tag[0] = "d0"
        mm([(R("pch", 0, Q), [(blk("id2", e), R("g2", e, AC), 2) for e in range(2)])])
        move(R("g4"), R("pch", 0, Q))
        add("V", lambda g: g.vector.tensor_tensor_scan(T.s1[:], T.one[:], T.cut[:], 0.0, A.mult, A.add),
            ["one", "cut"], ["s1"], vc(R("s1")))
        mm([(R("pm2", 64, 80), [(blk(z, e), R(x, e, 32), 2) for e in range(2) for z, x in (("be", "s1"), ("ue", "cut"))]),
            (R("pm2", 400, 401), [(bd, R("s1", 31, 32), 1)])])
        tt(R("t2"), R("jm"), R("pm2", 64, 80), A.min)
        ts(R("o2"), R("t2"), 2047.0, None, A.add)
        far, top, aim = R("sb", S, S + 12), R("pm2", 404, 416), R("pm2", 416, 428)
        ts(R("cnt"), R("pm2", 400, 401), g16, None, A.add)
        ts(far, R("jj", 0, 12), R("cnt"), 4.0 * V, A.is_ge, A.mult)
        scatter(R("cp"), R("o2"), R("g4"), ["cp"])
        pairs = [(R(("zc", "zd")[i % 2], 15 - i, 143 - i), R("cp", i // 2, S // 2), 8) for i in range(16)]
        mm([(top, pairs)])
        cp(R("to"), top)
        gather(R("sb", 0, S), cw, R("to"), CW)
        add("G", send, ["sb"], ["land"], (1000,), kind="r")
        tag[0] = "d1"
        mm([(aim, pairs + [(idp, far, 1)])], last=False)
        mm([(aim, [(blk("shd", d), R("land", W * d + S, W * d + S + 12), 1) for d in range(7)])], False)
        mm([(R("phb", 0, S), [(blk("shd", d), R("land", W * d, W * d + S), 1) for d in range(7)])])
        move(R("ar"), R("phb", 0, S))
        tt(R("t5"), R("j8", 32, 44), aim, A.min)
        cp(R("o3"), R("t5"))
        scatter(R("cw"), R("o3"), R("ar"), CW)
        tag[0] = "n"
        dma("G", [(T.nf[0:128:16, 0:V], T.nt[0:128:16, 0:V])], NT[:1] + ["land"], ["nf"], 1 << 18)
        dma("G", [(T.nf[0:128:16, 0:V], T.nt[1:128:16, 0:V])], NT[1:2], ["nf"], 1 << 19, accum_op=A.add, max_dma_last_dim=4096)

    def walk(r):
        for h in range(4 if r else 0):
            pw, tag[0] = PSUM[h], "w%d0%d" % (r, h)
            mm([(blk(pw, 1, Q), [(idp, blk("cd", 36 * r + h, Q), 1), (idn, blk("zz", 4 * r + h, Q), 1)])])
            move(blk("dd", h, Q), blk(pw, 1, Q))
            tag[0] = "p%d0%d" % (r, h)
            mm([(R(pw, 0, 64), fold("zw", "zz", 4 * r + h))])
            cp(blk("cq", h, 64), R(pw, 0, 64))
            ts(blk("cq", 4 + h, 64), blk("cq", h, 64), 7, None, A.bitwise_and)
            for s in pens:
                ts(blk("pen", 4 * s + h, 64), blk("cq", 4 + h, 64), s - 1.0, 32.0, A.is_lt, A.mult)
        for s in range(1, 9):
            for h in range(4):
                pw, tag[0] = PSUM[h], "b%d%d%d" % (r, s, h)
                d, b, rr, fs, pd = blk("dd", h, Q), blk("bb", h, Q), blk("rr", h, Q), blk("fs", h, 64), blk(pw, 1, Q)
                ts(b, d, 0.5, 0.5, A.is_gt, A.subtract)
                act(b, d, F.Sign, bias=-0.5)
                either()
                pen = [(idn, blk("pen", 4 * s + h, 64), 1)] if r and s in pens else []
                mm([(R(pw, 0, 64), pen + fold("zs", "bb", h))])
                tag[0] = "f%d%d%d" % (r, s, h)
                ts(fs, R(pw, 0, 64), thr, 2.0, A.is_lt, A.mult)
                act(fs, R(pw, 0, 64), F.Sign, bias=thr, scale=-1.0)
                either()
                tag[0], k = "w%d%d%d" % (r, s, h), 36 * r + 4 * s + h
                old = [(idn, d, 1), (idn, blk("zz", h, Q), 1)] if (r, s) == (0, 1) else [(idn, blk("cd", k - 4, Q), 1)]
                mm([(pd, old + [(idp, blk("cd", k, Q), 1)])])
                mm([(blk(pw, i, 64), [(blk("selt", i), fs, 1)]) for i in range(4)])
                tt(rr, d, blk(pw, 0, Q), A.mult)
                if s < 8:
                    tt(d, rr, pd, A.add)
                else:
                    z = blk("zz", 4 * r + 4 + h, Q)
                    tt(blk("db", h, Q), rr, pd, A.add)
                    act(z, blk("db", h, Q), F.Abs)
                    if r:
                        dma("Y", [(T.yz[:, Q * h:Q * h + Q], ap(z))], [z], ["yz%d" % h], 1 << 16)

    turns(0)
    chase(0, range(1, 9))
    cards(0, range(1, 9))
    cuts(0)
    cards(0, [9])
    deal()
    chase(1, range(1, raw + 2))
    walk(0)
    turns(1)
    chase(1, range(raw + 2, 9))
    cards(1, range(1, 9))
    cuts(1)
    cards(1, [9])
    tag[0] = "y"
    dma("Y", [(T.yn[:], T.nf[0:128:16, 0:V])], ["nf"], ["yn"], 1 << 18)
    dma("G", [(T.yc[:], T.g2[0:128:16, L:2 * L])], [R("g2", L, 2 * L)], ["yc"], 1 << 15)
    dma("G", [(T.yc[:], T.g2[1:128:16, L:2 * L])], [R("g2", L, 2 * L)], ["yc"], 1 << 16, accum_op=A.add, max_dma_last_dim=4096)
    walk(1)
    return ops


def depend(ops):
    hist, deps, above = {}, [], []
    for n, o in enumerate(ops):
        ds = set()
        for kind, rs in (("r", o["rd"]), ("w", o["wr"])):
            for name, a, b in rs:
                for m, k2, a2, b2 in hist.get(name, []):
                    if a < b2 and a2 < b and (kind == "w" or k2 == "w"):
                        ds.add(m)
        for kind, rs in (("r", o["rd"]), ("w", o["wr"])):
            for name, a, b in rs:
                h = hist.setdefault(name, [])
                if kind == "w":
                    h[:] = [e for e in h if not (a <= e[2] and e[3] <= b)]
                h.append((n, kind, a, b))
        above.append(ds.union(*[above[m] for m in ds]))
        deps.append([m for m in sorted(ds) if not any(m in above[j] for j in ds)])
    return deps


def followers(deps):
    succ = [[] for _ in deps]
    for k, d in enumerate(deps):
        for m in d:
            succ[m].append(k)
    return succ


def lengths(ops, tm):
    cost = [{q: tm["call"][q] + max(64, s[1]) * tm["cy"] if q in "VS" and s[1] else
             (tm["call"][q] if q == "P" else s[0]) + (s[1] + s[2] * tm["ga"] + s[3] * tm["sc"]) * tm["cy"] + s[4] * tm["pc"]
             for q, (_, s) in o["on"].items()} for o in ops]
    lat = [tm["dma"] + o["nbytes"] / tm["rate"] if o["kind"] == "d" else tm["send"] if o["kind"] == "r" else 0.0 for o in ops]
    return cost, lat


def place(ops, deps, tm):
    n, wake = len(ops), tm["wake"]
    cost, lat = lengths(ops, tm)
    deps = [d + [o["after"]] if "after" in o else d for d, o in zip(deps, ops)]
    succ, tail = followers(deps), [0.0] * n
    for k in range(n - 1, -1, -1):
        tail[k] = min(cost[k].values()) + lat[k] + wake + max([tail[j] for j in succ[k]] + [0.0])
    for k, o in enumerate(ops):
        tail[k] += o["pri"] + 100 * (URGE.get(o["tag"][:2], 0) - (STAGGER * int(o["tag"][3]) if o["tag"][0] in "bfw" else 0))
    left, busy, start, end, eng = [len(d) for d in deps], {}, [0.0] * n, [0.0] * n, [None] * n
    ready = [k for k in range(n) if not left[k]]
    while ready:
        k = max(ready, key=lambda x: (tail[x], -x))
        ready.remove(k)
        best = None
        for q, c in cost[k].items():
            t, again = max([end[m] + (0.0 if m == ops[k].get("after") else lat[m] + (tm["same"] if eng[m] == q else wake))
                            for m in deps[k]] + [0.0]), True
            while again:
                again = False
                for key in [q] + ops[k]["banks"]:
                    for a, b, q2 in busy.get(key, ()):
                        pad = 0.0 if key == q else wake
                        if a - pad < t + c and b + pad > t and (key == q or q2 != q):
                            t, again = b + pad, True
            v = t + c - (100 * LEAN.get(ops[k]["tag"][:2], 0) if q == "V" else 0)
            if best is None or v < best[0]:
                best = v, t, q
        start[k], eng[k] = best[1:]
        end[k] = start[k] + cost[k][eng[k]]
        for key in [eng[k]] + ops[k]["banks"]:
            busy[key] = sorted(busy.get(key, []) + [(start[k], end[k], eng[k])])
        for j in succ[k]:
            left[j] -= 1
            if not left[j]:
                ready.append(j)
    return sorted(range(n), key=lambda x: (start[x], x)), eng


def refine(ops, need, tms, order, eng, tries, heat, seed=1):
    n = len(ops)
    prec = [d + [o["after"]] if "after" in o else d for d, o in zip(need, ops)]
    succ, after = followers(prec), followers(need)
    banks, flex, rnd = [o["banks"] for o in ops], [k for k in range(n) if len(ops[k]["on"]) > 1], [seed]
    sizes = [lengths(ops, tm) + (tm["wake"], tm["wake"] - tm["same"]) for tm in tms]

    def pick(m):
        rnd[0] = (rnd[0] * 1103515245 + 12345) % 2147483648
        return (rnd[0] >> 8) % m

    def run(size, order, eng, first, last, limit, marks, end, why, rest):
        cost, lat, wake, near = size
        i0 = first // 32
        held, old, marks, end, why, reach = dict(marks[i0]), marks, marks[:i0], end[:], why[:], last
        for i in range(32 * i0, n):
            if i % 32 == 0:
                if i > reach and held == old[i // 32]:
                    marks += old[i // 32:]
                    break
                marks.append(dict(held))
            k = order[i]
            q = eng[k]
            t, _, w = held[q]
            for m in need[k]:
                e = end[m] - near if eng[m] == q else end[m]
                if e > t:
                    t, w = e, m
            for b in banks[k]:
                e = held[b]
                if e[1] != q and e[0] + wake > t:
                    t, w = e[0] + wake, e[2]
            if i > last and t + rest[k] > limit:
                return None
            t += cost[k][q]
            e = held[q] = (t, q, k)
            for b in banks[k]:
                held[b] = e
            t += lat[k] + wake
            if t != end[k]:
                end[k] = t
                for j in after[k]:
                    if pos[j] > reach:
                        reach = pos[j]
            why[k] = w
        top = max(end)
        return [top + 0.3 * sum(end) / n, top, marks, end, why]

    def back(size, order, eng):
        cost, lat, wake, near = size
        rest, nxt = [0.0] * n, {}
        for k in order[::-1]:
            q = eng[k]
            t = lat[k] + wake
            e = max(nxt.get(q, 0.0), t)
            for j in after[k]:
                x = t + rest[j] - near if eng[j] == q else t + rest[j]
                if x > e:
                    e = x
            for b in banks[k]:
                x = nxt.get(b)
                if x and x[1] != q and x[0] + wake > e:
                    e = x[0] + wake
            e = nxt[q] = rest[k] = cost[k][q] + e
            for b in banks[k]:
                nxt[b] = (e, q)
        return rest

    pos, taken = {x: i for i, x in enumerate(order)}, 0
    now = [run(s, order, eng, 0, n, 0, [{x: (0.0, x, None) for x in list("VSPGY") + PSUM}], [0.0] * n, [None] * n, None)
           + [back(s, order, eng)] for s in sizes]
    total = sum(x[0] for x in now)
    best, fresh, held_up = (total, order, eng), True, [(1, 0)]
    for it in range(tries):
        if fresh:
            one = now[pick(len(now))]
            k, chain = one[3].index(one[1]) if pick(10) >= 3 else pick(n), []
            while one[4][k] is not None:
                chain.append((one[4][k], k))
                k = one[4][k]
            held_up = [p for p in chain if p[0] not in need[p[1]]] or held_up
            loose = [p[1] for p in chain if len(ops[p[1]]["on"]) > 1] or flex
        o2, e2, kind, far, fresh = order, eng, pick(20), (0, 0, 0, 2, 5, 12, 30)[pick(7)], pick(30) == 0
        if kind < 3:
            k = flex[pick(len(flex))] if kind == 0 else loose[pick(len(loose))]
            e2, a, b = eng[:], pos[k], max([pos[k]] + [pos[j] for j in after[k]])
            e2[k] = "V" if eng[k] == "S" else "S"
        else:
            x, y = held_up[pick(len(held_up))]
            if pos[x] > pos[y]:
                continue
            up = kind < 12
            a, b = (max(0, pos[x] - far), pos[y]) if up else (pos[x], min(n - 1, pos[y] + far))
            seg, mv = order[a:b + 1], {y if up else x}
            for j in (seg[::-1] if up else seg):
                if any(m in mv for m in (succ if up else prec)[j]):
                    mv.add(j)
            if (x if up else y) in mv:
                continue
            o2 = order[:a] + [j for j in seg if (j in mv) == up] + [j for j in seg if (j in mv) != up] + order[b + 1:]
        room, new = heat * (1 - it / tries) * pick(1000) / 1000, []
        for s, old in zip(sizes, now):
            new.append(run(s, o2, e2, a, b, old[1] + 3 * room + 100, *old[2:]))
            if new[-1] is None:
                break
        if new[-1] and sum(x[0] for x in new) <= total + room * len(now):
            order, eng, fresh, total, taken = o2, e2, True, sum(x[0] for x in new), taken + 1
            now = [x + [back(s, order, eng) if taken % 8 == 0 else y[5]] for s, x, y in zip(sizes, new, now)]
            for i in range(a, b + 1):
                pos[order[i]] = i
            if total < best[0]:
                best = total, o2, e2
    return best[1:]


def plan(ops):
    if not PLAN:
        deps = depend(ops)
        got = place(ops, deps, dict(TIMES[0], cy=0.84, pc=0.40, ga=1.45, sc=3.2))
        for t in TRIES:
            got = refine(ops, deps, TIMES, *got, *t)
        PLAN["p"] = got + (deps,)
    return PLAN["p"]


def emit(g, T, ops, order, on, deps):
    eng = {"V": g.vector, "S": g.scalar, "P": g.tensor, "G": g, "Y": g.sync}
    count, know, token, last, pos = {}, {q: {} for q in eng}, {}, {}, {k: i for i, k in enumerate(order)}
    nd = 0
    for k in order:
        o, q = ops[k], on[k]
        fn = o["on"][q][0]
        need = list(deps[k])
        for b in o["banks"]:
            if b in last and on[last[b]] != q:
                need.append(last[b])
            last[b] = k
        for m in sorted(need, key=lambda x: -pos[x]):
            s, v, seen = token[m]
            if know[q].get(s, 0) < v:
                eng[q].wait_ge(T.sem[s], v)
                for s2 in seen:
                    know[q][s2] = max(know[q].get(s2, 0), seen[s2])
        if o["kind"] == "c":
            s = "q" + q
            fn(g).then_inc(T.sem[s], 1)
            v = count.get(s, 0) + 1
        elif o["kind"] == "d":
            s = "d%d" % nd
            nd += 1
            v = fn(g, T.sem[s])
        else:
            s = "arr"
            v = count["sent"] = fn(g)
        count[s] = v
        token[k] = (s, v, dict(know[q], **{s: v}))
    for s in count:
        g.sync.wait_ge(T.sem[s], count[s])


def sender(core, T, topo):
    rank, n = T.rank_of(core), len(T.cores)

    def send(g):
        peers = [T.cores[(rank + 1 + d) % n] for d in range(n - 1)]
        es = topo.engines(core, peers[0])
        far, near = list(es[0::2]), list(es[1::2])
        trs = []
        for d, p in enumerate(peers):
            pool = far if topo.die(p) != topo.die(core) else near
            rid, pid, _ = topo.addr(p)
            trs.append(RemoteDMATransfer(dst_ids=[DstId(rid=rid, pnc=pid)], dma_engine_mask=(1 << pool.pop()) | (1 << pool.pop()),
                                         remote_sem=T.sem.arr, src=T.sb[:], dst=T.land[:, W * d:W * d + W]))
        g.remote_dma_fused(trs, local_sem=T.sem.sent)
        return 2 * len(peers)
    return send


def rank_program(g, core, T, topo):
    if T.rank_of(core) is None:
        return
    ops = build(T, sender(core, T, topo))
    emit(g, T, ops, *plan(ops))
